import numpy as np
import ml_dtypes


def mxq(x, axis, fmt="e4m3"):
    dtype, down = {"e4m3": (ml_dtypes.float8_e4m3fn, 7), "e5m2": (ml_dtypes.float8_e5m2, 14)}[fmt]
    v = np.moveaxis(np.asarray(x, np.float32).astype(ml_dtypes.bfloat16).astype(np.float64), axis, -1)
    blocks = v.reshape(v.shape[:-1] + (-1, 32))
    amax = np.abs(blocks).max(-1, keepdims=True)
    byte = np.maximum(np.where(amax > 0, np.frexp(amax)[1] - 1 + 127, 0) - down, 1)
    scale = np.exp2(byte - 127.0)
    codes = (blocks / scale).astype(np.float32).astype(dtype).astype(np.float64)
    return np.moveaxis((codes * scale).reshape(v.shape), -1, axis)


WIDE = False


def mx_kscale(k):
    if not WIDE:
        return np.ones(k)
    levels = np.array([10, -10, 5, -5, 0])
    if k % 512:
        return np.exp2(np.random.permutation(np.resize(levels, k // 32))).repeat(32)
    a = np.empty((k // 512, 16))
    for p in range(k // 512):
        a[p, :8] = np.random.permutation(np.resize(levels, 8))
        for g in range(8):
            far = levels[np.abs(levels - a[p, g]) >= 10]
            a[p, g + 8] = far[np.random.randint(len(far))]
    return np.exp2(a.ravel()).repeat(32)


def f64(x):
    return np.asarray(x).astype(np.float64)


def striped(idx):
    return np.tile(idx.reshape(-1, 16).T, (8, 1)).astype(np.uint16)


def unstriped(offs):
    return offs[:16].T.reshape(-1).astype(np.int64)


def pack_weight(w):
    k, n = w.shape
    w = f64(np.asarray(w, np.float32).astype(ml_dtypes.bfloat16)).reshape(k // 32, 32, n)
    amax = np.abs(w).max(1)
    byte = np.clip(np.where(amax > 0, np.frexp(amax)[1] - 1 + 127 - 7, 1), 1, 254)
    scaled = (w * np.exp2(127.0 - byte)[:, None, :]).reshape(k, n).astype(np.float32)
    words = np.ascontiguousarray(scaled.reshape(k // 512, 128, 4, n).transpose(0, 1, 3, 2)).astype(ml_dtypes.float8_e4m3fn).view(np.uint8)
    return words, np.ascontiguousarray(byte.astype(np.uint8).reshape(k // 512, 16, n))


def unpack_weight(words, scales):
    g, p, n, _ = words.shape
    vals = np.ascontiguousarray(words).view(ml_dtypes.float8_e4m3fn).astype(np.float64) * np.repeat(np.exp2(scales.astype(np.float64) - 127.0), 8, axis=1)[..., None]
    return vals.transpose(0, 1, 3, 2).reshape(g * 512, n)


K, T, S, N, U = 512, 4096, 1024, 128, 2048


def setup_inputs():
    n = np.random.standard_normal
    s = mx_kscale(K)[:, None]
    packed_xT = pack_weight(n((K, T)) * s)
    return {
        "x_words": packed_xT[0],
        "x_scales": packed_xT[1],
        "mem": n((N, U)).astype(np.float32),
        "w1": (n((K, N)) / np.sqrt(K) / s).astype(np.float32),
        "offs": striped(np.random.permutation(T)[:S]),
        "slot": striped(np.random.permutation(U)[:S]),
    }


def reference(x_words, x_scales, mem, w1, offs, slot):
    xq = unpack_weight(x_words, x_scales)[:, unstriped(offs)]
    y = np.tanh(mxq(f64(w1), 0, "e4m3").T @ xq)
    out = f64(mem).copy()
    out[:, unstriped(slot)] = y
    return out

@@ -1,0 +1,82 @@
+from contextlib import ExitStack
+
+import concourse.mybir as mybir
+
+K, T, S, N, U = 512, 4096, 1024, 128, 2048
+FLOPS = 2 * K * N * S
+
+F32 = mybir.dt.float32
+BF16 = mybir.dt.bfloat16
+I32 = mybir.dt.int32
+U32 = mybir.dt.uint32
+U16 = mybir.dt.uint16
+U8 = mybir.dt.uint8
+FP8X4 = mybir.dt.float8_e4m3fn_x4
+TANH = mybir.ActivationFunctionType.Tanh
+
+P = 128
+PACK = 4
+STRIPE = 16
+HALF = 512
+PIECE = 256
+
+
+def tile_picked_kvput_tanh_p_kernel(tc, x_words, x_scales, mem, w1, offs, slot, out):
+    nc = tc.nc
+    with ExitStack() as ctx:
+        keep = ctx.enter_context(tc.tile_pool(name="keep", bufs=1))
+        psum = ctx.enter_context(tc.psum_pool(name="psum", bufs=1))
+
+        offs_sb = keep.tile([P, S // STRIPE], U16, name="offs_sb")
+        slot_sb = keep.tile([P, S // STRIPE], U16, name="slot_sb")
+        words = keep.tile([P, T], U32, name="words", align_bytes=64)
+        scales = keep.tile([P, T], U8, name="scales", tag="scales_then_picked", align_bytes=64)
+        w_raw = keep.tile([P, PACK, N], F32, name="w_raw", align_bytes=64)
+        window = keep.tile([P, U], F32, name="window", align_bytes=64)
+
+        nc.vector.memset(scales[:].bitcast(I32), 0)
+        warm = keep.tile([P, 8], F32, name="warm")
+        warm_out = keep.tile([P, 8], F32, name="warm_out")
+        nc.gpsimd.memset(warm[:], 0.0)
+
+        nc.sync.dma_start(offs_sb[:], offs)
+        nc.sync.dma_start(w_raw[:], w1.rearrange("(p j) m -> p j m", j=PACK))
+        nc.sync.dma_start(words[:].bitcast(I32), x_words[0].rearrange("p n t -> p (n t)").bitcast(I32), max_dma_last_dim=4096)
+        scale_rows = x_scales[0].bitcast(I32).rearrange("(q r) n -> r q n", r=4)
+        for r in range(4):
+            nc.scalar.dma_start(scales[r:P:32, :].bitcast(I32), scale_rows[r])
+        nc.scalar.activation(warm_out[:], warm[:], TANH)
+        nc.sync.dma_start(slot_sb[:], slot)
+        nc.sync.dma_start(window[:], mem)
+
+        w_grouped = keep.tile([P, N, PACK], BF16, name="w_grouped", align_bytes=64)
+        w_codes = keep.tile([P, N], U32, name="w_codes", align_bytes=64)
+        w_scales = keep.tile([P, N], U8, name="w_scales", align_bytes=64)
+        nc.vector.tensor_copy(out=w_grouped[:], in_=w_raw[:].rearrange("p j m -> p m j"))
+
+        picked_scales = keep.tile([P, S], U8, name="picked_scales", align_bytes=64)
+        nc.vector.tensor_copy(picked_scales[:], scales[:].indirect(offs_sb[:]))
+        nc.vector.quantize_mx(out=w_codes[:].bitcast(FP8X4), scales=w_scales[:], in_=w_grouped[:].rearrange("p m j -> p (m j)"))
+
+        y = keep.tile([P, S], F32, name="y", align_bytes=64)
+        for h in range(S // HALF):
+            picked = keep.tile([P, HALF], U32, name="picked%d" % h, tag=("scales_then_picked", "picked1")[h], align_bytes=64)
+            cols = slice(h * HALF // STRIPE, (h + 1) * HALF // STRIPE)
+            nc.vector.tensor_copy(picked[:], words[:].indirect(offs_sb[:, cols]))
+            for c in range(HALF // PIECE):
+                j0 = h * HALF + c * PIECE
+                acc = psum.tile([P, PIECE], F32, name="acc%d" % (j0 // PIECE))
+                nc.tensor.matmul_mx(
+                    out=acc[:],
+                    lhsT=w_codes[:].bitcast(FP8X4),
+                    lhsT_scale=w_scales[:],
+                    rhs=picked[:, c * PIECE : (c + 1) * PIECE].bitcast(FP8X4),
+                    rhs_scale=picked_scales[:, j0 : j0 + PIECE],
+                    start=True,
+                    stop=True,
+                )
+                nc.scalar.activation(y[:, j0 : j0 + PIECE], acc[:], TANH)
+
+        for j0, j1 in ((0, PIECE), (PIECE, S)):
+            nc.vector.tensor_copy(window[:].indirect(slot_sb[:, j0 // STRIPE : j1 // STRIPE]), y[:, j0:j1])
+        nc.sync.dma_start(out, window[:])

@@ -16,67 +16,97 @@ TANH = mybir.ActivationFunctionType.Tanh
 
 P = 128
 PACK = 4
+QUADRANT = 32
+PLANE_ROWS = 4
 STRIPE = 16
-HALF = 512
-PIECE = 256
+ALIGN = 64
+
+SPREAD_START, SPREAD_STEP = 4, 8
+
+HALF = S // 2
+FIRST = 256
+PRODUCTS = (((0, FIRST // 2), (FIRST // 2, FIRST), (FIRST, HALF)), ((HALF, HALF + FIRST), (HALF + FIRST, S)))
+WORD_DESCRIPTOR_BYTES = 8192
 
 
 def tile_picked_kvput_tanh_p_kernel(tc, x_words, x_scales, mem, w1, offs, slot, out):
     nc = tc.nc
     with ExitStack() as ctx:
         keep = ctx.enter_context(tc.tile_pool(name="keep", bufs=1))
+        reused = ctx.enter_context(tc.tile_pool(name="reused", bufs=1))
         psum = ctx.enter_context(tc.psum_pool(name="psum", bufs=1))
 
         offs_sb = keep.tile([P, S // STRIPE], U16, name="offs_sb")
         slot_sb = keep.tile([P, S // STRIPE], U16, name="slot_sb")
-        words = keep.tile([P, T], U32, name="words", align_bytes=64)
-        scales = keep.tile([P, T], U8, name="scales", tag="scales_then_picked", align_bytes=64)
-        w_raw = keep.tile([P, PACK, N], F32, name="w_raw", align_bytes=64)
-        window = keep.tile([P, U], F32, name="window", align_bytes=64)
+        words = keep.tile([P, T], U32, name="words", align_bytes=ALIGN)
+        scales = keep.tile([P, T], U8, name="scales", align_bytes=ALIGN)
+        w_raw = keep.tile([P, PACK, N], F32, name="w_raw", align_bytes=ALIGN)
 
         nc.vector.memset(scales[:].bitcast(I32), 0)
-        warm = keep.tile([P, 8], F32, name="warm")
-        warm_out = keep.tile([P, 8], F32, name="warm_out")
-        nc.gpsimd.memset(warm[:], 0.0)
 
         nc.sync.dma_start(offs_sb[:], offs)
         nc.sync.dma_start(w_raw[:], w1.rearrange("(p j) m -> p j m", j=PACK))
-        nc.sync.dma_start(words[:].bitcast(I32), x_words[0].rearrange("p n t -> p (n t)").bitcast(I32), max_dma_last_dim=4096)
-        scale_rows = x_scales[0].bitcast(I32).rearrange("(q r) n -> r q n", r=4)
-        for r in range(4):
-            nc.scalar.dma_start(scales[r:P:32, :].bitcast(I32), scale_rows[r])
-        nc.scalar.activation(warm_out[:], warm[:], TANH)
         nc.sync.dma_start(slot_sb[:], slot)
+        nc.sync.dma_start(scales[SPREAD_START:P:SPREAD_STEP, :].bitcast(I32), x_scales[0].bitcast(I32))
+        nc.sync.dma_start(
+            words[:].bitcast(I32),
+            x_words[0].rearrange("p n t -> p (n t)").bitcast(I32),
+            max_dma_last_dim=WORD_DESCRIPTOR_BYTES,
+        )
+
+        w_grouped = reused.tile([P, N, PACK], BF16, name="w_grouped", align_bytes=ALIGN, offset=0)
+        w_codes = keep.tile([P, N], U32, name="w_codes", align_bytes=ALIGN)
+        w_plane = keep.tile([P, N], U8, name="w_plane", align_bytes=ALIGN)
+        nc.scalar.copy(out=w_grouped[:], in_=w_raw[:].rearrange("p j m -> p m j"))
+
+        x_plane = keep.tile([P, S], U8, name="x_plane", align_bytes=ALIGN)
+        nc.vector.memset(x_plane[:].bitcast(I32), 0)
+
+        def entries(list_tile, j0, j1):
+            return list_tile[:, j0 // STRIPE : j1 // STRIPE]
+
+        def pick_scales(h, spread, last_queue):
+            j0, j1 = h * HALF, (h + 1) * HALF
+            nc.vector.tensor_copy(spread[:], scales[:].indirect(entries(offs_sb, j0, j1)))
+            for r in range(PLANE_ROWS):
+                queue = last_queue if r == PLANE_ROWS - 1 else nc.sync
+                queue.dma_start(
+                    x_plane[r:P:QUADRANT, j0:j1].bitcast(I32),
+                    spread[SPREAD_START + SPREAD_STEP * r : P : QUADRANT, :].bitcast(I32),
+                )
+
+        spread_first = keep.tile([P, HALF], U8, name="spread_first", align_bytes=ALIGN)
+        pick_scales(0, spread_first, nc.scalar)
+        nc.vector.quantize_mx(
+            out=w_codes[:].bitcast(FP8X4),
+            scales=w_plane[:],
+            in_=w_grouped[:].rearrange("p m j -> p (m j)"),
+        )
+        window = reused.tile([P, U], F32, name="window", align_bytes=ALIGN, offset=HALF)
+        spread_second = reused.tile([P, HALF], U8, name="spread_second", align_bytes=ALIGN, offset=0)
         nc.sync.dma_start(window[:], mem)
+        pick_scales(1, spread_second, nc.sync)
 
-        w_grouped = keep.tile([P, N, PACK], BF16, name="w_grouped", align_bytes=64)
-        w_codes = keep.tile([P, N], U32, name="w_codes", align_bytes=64)
-        w_scales = keep.tile([P, N], U8, name="w_scales", align_bytes=64)
-        nc.vector.tensor_copy(out=w_grouped[:], in_=w_raw[:].rearrange("p j m -> p m j"))
-
-        picked_scales = keep.tile([P, S], U8, name="picked_scales", align_bytes=64)
-        nc.vector.tensor_copy(picked_scales[:], scales[:].indirect(offs_sb[:]))
-        nc.vector.quantize_mx(out=w_codes[:].bitcast(FP8X4), scales=w_scales[:], in_=w_grouped[:].rearrange("p m j -> p (m j)"))
-
-        y = keep.tile([P, S], F32, name="y", align_bytes=64)
+        y_first = keep.tile([P, FIRST], F32, name="y_first", align_bytes=ALIGN)
+        y_rest = keep.tile([P, S - FIRST], F32, name="y_rest", align_bytes=ALIGN)
+        picked = keep.tile([P, S], U32, name="picked", align_bytes=ALIGN)
         for h in range(S // HALF):
-            picked = keep.tile([P, HALF], U32, name="picked%d" % h, tag=("scales_then_picked", "picked1")[h], align_bytes=64)
-            cols = slice(h * HALF // STRIPE, (h + 1) * HALF // STRIPE)
-            nc.vector.tensor_copy(picked[:], words[:].indirect(offs_sb[:, cols]))
-            for c in range(HALF // PIECE):
-                j0 = h * HALF + c * PIECE
-                acc = psum.tile([P, PIECE], F32, name="acc%d" % (j0 // PIECE))
+            h0, h1 = h * HALF, (h + 1) * HALF
+            nc.vector.tensor_copy(picked[:, h0:h1], words[:].indirect(entries(offs_sb, h0, h1)))
+            for j0, j1 in PRODUCTS[h]:
+                acc = psum.tile([P, j1 - j0], F32, name="acc%d" % j0)
                 nc.tensor.matmul_mx(
                     out=acc[:],
                     lhsT=w_codes[:].bitcast(FP8X4),
-                    lhsT_scale=w_scales[:],
-                    rhs=picked[:, c * PIECE : (c + 1) * PIECE].bitcast(FP8X4),
-                    rhs_scale=picked_scales[:, j0 : j0 + PIECE],
+                    lhsT_scale=w_plane[:],
+                    rhs=picked[:, j0:j1].bitcast(FP8X4),
+                    rhs_scale=x_plane[:, j0:j1],
                     start=True,
                     stop=True,
                 )
-                nc.scalar.activation(y[:, j0 : j0 + PIECE], acc[:], TANH)
+                y = y_first[:, j0:j1] if j0 < FIRST else y_rest[:, j0 - FIRST : j1 - FIRST]
+                nc.scalar.activation(y, acc[:], TANH)
 
-        for j0, j1 in ((0, PIECE), (PIECE, S)):
-            nc.vector.tensor_copy(window[:].indirect(slot_sb[:, j0 // STRIPE : j1 // STRIPE]), y[:, j0:j1])
+        nc.vector.tensor_copy(window[:].indirect(entries(slot_sb, 0, FIRST)), y_first[:])
+        nc.vector.tensor_copy(window[:].indirect(entries(slot_sb, FIRST, S)), y_rest[:])
         nc.sync.dma_start(out, window[:])

@@ -21,7 +21,8 @@ PLANE_ROWS = 4
 STRIPE = 16
 ALIGN = 64
 
-SPREAD_START, SPREAD_STEP = 4, 8
+SPREAD_START, SPREAD_STEP = 32, 4
+SCALE_ROWS = 16
 
 HALF = S // 2
 FIRST = 256
@@ -47,7 +48,7 @@ def tile_picked_kvput_tanh_p_kernel(tc, x_words, x_scales, mem, w1, offs, slot, 
         nc.sync.dma_start(offs_sb[:], offs)
         nc.sync.dma_start(w_raw[:], w1.rearrange("(p j) m -> p j m", j=PACK))
         nc.sync.dma_start(slot_sb[:], slot)
-        nc.sync.dma_start(scales[SPREAD_START:P:SPREAD_STEP, :].bitcast(I32), x_scales[0].bitcast(I32))
+        nc.sync.dma_start(scales[SPREAD_START : SPREAD_START + SPREAD_STEP * SCALE_ROWS : SPREAD_STEP, :].bitcast(I32), x_scales[0].bitcast(I32))
         nc.sync.dma_start(
             words[:].bitcast(I32),
             x_words[0].rearrange("p n t -> p (n t)").bitcast(I32),
@@ -72,7 +73,9 @@ def tile_picked_kvput_tanh_p_kernel(tc, x_words, x_scales, mem, w1, offs, slot, 
                 queue = last_queue if r == PLANE_ROWS - 1 else nc.sync
                 queue.dma_start(
                     x_plane[r:P:QUADRANT, j0:j1].bitcast(I32),
-                    spread[SPREAD_START + SPREAD_STEP * r : P : QUADRANT, :].bitcast(I32),
+                    spread[
+                        SPREAD_START + SPREAD_STEP * r : SPREAD_START + SPREAD_STEP * SCALE_ROWS : SPREAD_STEP * PLANE_ROWS, :
+                    ].bitcast(I32),
                 )
 
         spread_first = keep.tile([P, HALF], U8, name="spread_first", align_bytes=ALIGN)

@@ -27,7 +27,6 @@ SCALE_ROWS = 16
 HALF = S // 2
 FIRST = 256
 PRODUCTS = (((0, FIRST // 2), (FIRST // 2, FIRST), (FIRST, HALF)), ((HALF, HALF + FIRST), (HALF + FIRST, S)))
-WORD_DESCRIPTOR_BYTES = 8192
 
 
 def tile_picked_kvput_tanh_p_kernel(tc, x_words, x_scales, mem, w1, offs, slot, out):
@@ -52,7 +51,6 @@ def tile_picked_kvput_tanh_p_kernel(tc, x_words, x_scales, mem, w1, offs, slot, 
         nc.sync.dma_start(
             words[:].bitcast(I32),
             x_words[0].rearrange("p n t -> p (n t)").bitcast(I32),
-            max_dma_last_dim=WORD_DESCRIPTOR_BYTES,
         )
 
         w_grouped = reused.tile([P, N, PACK], BF16, name="w_grouped", align_bytes=ALIGN, offset=0)

@@ -20,6 +20,7 @@ QUADRANT = 32
 PLANE_ROWS = 4
 STRIPE = 16
 ALIGN = 64
+DMA_ALIGN = 256
 
 SPREAD_START, SPREAD_STEP = 32, 4
 SCALE_ROWS = 16
@@ -38,9 +39,9 @@ def tile_picked_kvput_tanh_p_kernel(tc, x_words, x_scales, mem, w1, offs, slot, 
 
         offs_sb = keep.tile([P, S // STRIPE], U16, name="offs_sb")
         slot_sb = keep.tile([P, S // STRIPE], U16, name="slot_sb")
-        words = keep.tile([P, T], U32, name="words", align_bytes=ALIGN)
-        scales = keep.tile([P, T], U8, name="scales", align_bytes=ALIGN)
-        w_raw = keep.tile([P, PACK, N], F32, name="w_raw", align_bytes=ALIGN)
+        words = keep.tile([P, T], U32, name="words", align_bytes=DMA_ALIGN)
+        scales = keep.tile([P, T], U8, name="scales", align_bytes=DMA_ALIGN)
+        w_raw = keep.tile([P, PACK, N], F32, name="w_raw", align_bytes=DMA_ALIGN)
 
         nc.vector.memset(scales[:].bitcast(I32), 0)
 
@@ -83,7 +84,7 @@ def tile_picked_kvput_tanh_p_kernel(tc, x_words, x_scales, mem, w1, offs, slot, 
             scales=w_plane[:],
             in_=w_grouped[:].rearrange("p m j -> p (m j)"),
         )
-        window = reused.tile([P, U], F32, name="window", align_bytes=ALIGN, offset=HALF)
+        window = reused.tile([P, U], F32, name="window", align_bytes=DMA_ALIGN, offset=HALF)
         spread_second = reused.tile([P, HALF], U8, name="spread_second", align_bytes=ALIGN, offset=0)
         nc.sync.dma_start(window[:], mem)
         pick_scales(1, spread_second, nc.sync)

@@ -27,7 +27,7 @@ SCALE_ROWS = 16
 
 HALF = S // 2
 FIRST = 256
-PRODUCTS = (((0, FIRST // 2), (FIRST // 2, FIRST), (FIRST, HALF)), ((HALF, HALF + FIRST), (HALF + FIRST, S)))
+PRODUCTS = (((0, FIRST // 2), (FIRST // 2, FIRST), (FIRST, HALF)), tuple((j, j + N) for j in range(HALF, S, N)))
 
 
 def tile_picked_kvput_tanh_p_kernel(tc, x_words, x_scales, mem, w1, offs, slot, out):
@@ -65,11 +65,11 @@ def tile_picked_kvput_tanh_p_kernel(tc, x_words, x_scales, mem, w1, offs, slot, 
         def entries(list_tile, j0, j1):
             return list_tile[:, j0 // STRIPE : j1 // STRIPE]
 
-        def pick_scales(h, spread, last_queue):
+        def pick_scales(h, spread, on_sync):
             j0, j1 = h * HALF, (h + 1) * HALF
             nc.vector.tensor_copy(spread[:], scales[:].indirect(entries(offs_sb, j0, j1)))
             for r in range(PLANE_ROWS):
-                queue = last_queue if r == PLANE_ROWS - 1 else nc.sync
+                queue = nc.sync if r < on_sync else nc.scalar
                 queue.dma_start(
                     x_plane[r:P:QUADRANT, j0:j1].bitcast(I32),
                     spread[
@@ -78,7 +78,7 @@ def tile_picked_kvput_tanh_p_kernel(tc, x_words, x_scales, mem, w1, offs, slot, 
                 )
 
         spread_first = keep.tile([P, HALF], U8, name="spread_first", align_bytes=ALIGN)
-        pick_scales(0, spread_first, nc.scalar)
+        pick_scales(0, spread_first, 3)
         nc.vector.quantize_mx(
             out=w_codes[:].bitcast(FP8X4),
             scales=w_plane[:],
@@ -87,7 +87,7 @@ def tile_picked_kvput_tanh_p_kernel(tc, x_words, x_scales, mem, w1, offs, slot, 
         window = reused.tile([P, U], F32, name="window", align_bytes=DMA_ALIGN, offset=HALF)
         spread_second = reused.tile([P, HALF], U8, name="spread_second", align_bytes=ALIGN, offset=0)
         nc.sync.dma_start(window[:], mem)
-        pick_scales(1, spread_second, nc.sync)
+        pick_scales(1, spread_second, 2)
 
         y_first = keep.tile([P, FIRST], F32, name="y_first", align_bytes=ALIGN)
         y_rest = keep.tile([P, S - FIRST], F32, name="y_rest", align_bytes=ALIGN)

@@ -43,16 +43,20 @@ def tile_picked_kvput_tanh_p_kernel(tc, x_words, x_scales, mem, w1, offs, slot, 
         scales = keep.tile([P, T], U8, name="scales", align_bytes=DMA_ALIGN)
         w_raw = keep.tile([P, PACK, N], F32, name="w_raw", align_bytes=DMA_ALIGN)
 
-        nc.vector.memset(scales[:].bitcast(I32), 0)
+        scale_words = scales[:].bitcast(I32)
+        nc.vector.memset(scale_words[:, :261], 0)
+        nc.vector.memset(scale_words[:, 261:520], 0)
+        nc.gpsimd.memset(scale_words[:, 520:], 0)
 
         nc.sync.dma_start(offs_sb[:], offs)
         nc.sync.dma_start(w_raw[:], w1.rearrange("(p j) m -> p j m", j=PACK))
-        nc.sync.dma_start(slot_sb[:], slot)
         nc.sync.dma_start(scales[SPREAD_START : SPREAD_START + SPREAD_STEP * SCALE_ROWS : SPREAD_STEP, :].bitcast(I32), x_scales[0].bitcast(I32))
         nc.sync.dma_start(
             words[:].bitcast(I32),
             x_words[0].rearrange("p n t -> p (n t)").bitcast(I32),
         )
+
+        nc.sync.dma_start(slot_sb[:], slot)
 
         w_grouped = reused.tile([P, N, PACK], BF16, name="w_grouped", align_bytes=ALIGN, offset=0)
         w_codes = keep.tile([P, N], U32, name="w_codes", align_bytes=ALIGN)
@@ -87,7 +91,7 @@ def tile_picked_kvput_tanh_p_kernel(tc, x_words, x_scales, mem, w1, offs, slot, 
         window = reused.tile([P, U], F32, name="window", align_bytes=DMA_ALIGN, offset=HALF)
         spread_second = reused.tile([P, HALF], U8, name="spread_second", align_bytes=ALIGN, offset=0)
         nc.sync.dma_start(window[:], mem)
-        pick_scales(1, spread_second, 2)
+        pick_scales(1, spread_second, 4)
 
         y_first = keep.tile([P, FIRST], F32, name="y_first", align_bytes=ALIGN)
         y_rest = keep.tile([P, S - FIRST], F32, name="y_rest", align_bytes=ALIGN)

@@ -26,8 +26,8 @@ SPREAD_START, SPREAD_STEP = 32, 4
 SCALE_ROWS = 16
 
 HALF = S // 2
-FIRST = 256
-PRODUCTS = (((0, FIRST // 2), (FIRST // 2, FIRST), (FIRST, HALF)), tuple((j, j + N) for j in range(HALF, S, N)))
+FIRST = 192
+PRODUCTS = (((0, N), (N, FIRST), (FIRST, 2 * N), (2 * N, HALF)), tuple((j, j + N) for j in range(HALF, S, N)))
 
 
 def tile_picked_kvput_tanh_p_kernel(tc, x_words, x_scales, mem, w1, offs, slot, out):
@@ -65,6 +65,8 @@ def tile_picked_kvput_tanh_p_kernel(tc, x_words, x_scales, mem, w1, offs, slot, 
 
         x_plane = keep.tile([P, S], U8, name="x_plane", align_bytes=ALIGN)
         nc.vector.memset(x_plane[:].bitcast(I32), 0)
+        zeros = keep.tile([P, FIRST], F32, name="zeros", align_bytes=ALIGN)
+        nc.vector.memset(zeros[:], 0.0)
 
         def entries(list_tile, j0, j1):
             return list_tile[:, j0 // STRIPE : j1 // STRIPE]
@@ -113,6 +115,6 @@ def tile_picked_kvput_tanh_p_kernel(tc, x_words, x_scales, mem, w1, offs, slot, 
                 y = y_first[:, j0:j1] if j0 < FIRST else y_rest[:, j0 - FIRST : j1 - FIRST]
                 nc.scalar.activation(y, acc[:], TANH)
 
-        nc.vector.tensor_copy(window[:].indirect(entries(slot_sb, 0, FIRST)), y_first[:])
+        nc.vector.tensor_tensor(window[:].indirect(entries(slot_sb, 0, FIRST)), y_first[:], zeros[:], mybir.AluOpType.add)
         nc.vector.tensor_copy(window[:].indirect(entries(slot_sb, FIRST, S)), y_rest[:])
         nc.sync.dma_start(out, window[:])

@@ -44,9 +44,9 @@ def tile_picked_kvput_tanh_p_kernel(tc, x_words, x_scales, mem, w1, offs, slot, 
         w_raw = keep.tile([P, PACK, N], F32, name="w_raw", align_bytes=DMA_ALIGN)
 
         scale_words = scales[:].bitcast(I32)
-        nc.vector.memset(scale_words[:, :261], 0)
-        nc.vector.memset(scale_words[:, 261:520], 0)
-        nc.gpsimd.memset(scale_words[:, 520:], 0)
+        nc.vector.memset(scale_words[:, :209], 0)
+        nc.vector.memset(scale_words[:, 209:416], 0)
+        nc.gpsimd.memset(scale_words[:, 416:], 0)
 
         nc.sync.dma_start(offs_sb[:], offs)
         nc.sync.dma_start(w_raw[:], w1.rearrange("(p j) m -> p j m", j=PACK))

@@ -71,12 +71,11 @@ def tile_picked_kvput_tanh_p_kernel(tc, x_words, x_scales, mem, w1, offs, slot, 
         def entries(list_tile, j0, j1):
             return list_tile[:, j0 // STRIPE : j1 // STRIPE]
 
-        def pick_scales(h, spread, on_sync):
+        def pick_scales(h, spread):
             j0, j1 = h * HALF, (h + 1) * HALF
             nc.vector.tensor_copy(spread[:], scales[:].indirect(entries(offs_sb, j0, j1)))
             for r in range(PLANE_ROWS):
-                queue = nc.sync if r < on_sync else nc.scalar
-                queue.dma_start(
+                nc.sync.dma_start(
                     x_plane[r:P:QUADRANT, j0:j1].bitcast(I32),
                     spread[
                         SPREAD_START + SPREAD_STEP * r : SPREAD_START + SPREAD_STEP * SCALE_ROWS : SPREAD_STEP * PLANE_ROWS, :
@@ -84,7 +83,7 @@ def tile_picked_kvput_tanh_p_kernel(tc, x_words, x_scales, mem, w1, offs, slot, 
                 )
 
         spread_first = keep.tile([P, HALF], U8, name="spread_first", align_bytes=ALIGN)
-        pick_scales(0, spread_first, 3)
+        pick_scales(0, spread_first)
         nc.vector.quantize_mx(
             out=w_codes[:].bitcast(FP8X4),
             scales=w_plane[:],
@@ -93,7 +92,7 @@ def tile_picked_kvput_tanh_p_kernel(tc, x_words, x_scales, mem, w1, offs, slot, 
         window = reused.tile([P, U], F32, name="window", align_bytes=DMA_ALIGN, offset=HALF)
         spread_second = reused.tile([P, HALF], U8, name="spread_second", align_bytes=ALIGN, offset=0)
         nc.sync.dma_start(window[:], mem)
-        pick_scales(1, spread_second, 4)
+        pick_scales(1, spread_second)
 
         y_first = keep.tile([P, FIRST], F32, name="y_first", align_bytes=ALIGN)
         y_rest = keep.tile([P, S - FIRST], F32, name="y_rest", align_bytes=ALIGN)

@@ -26,8 +26,8 @@ SPREAD_START, SPREAD_STEP = 32, 4
 SCALE_ROWS = 16
 
 HALF = S // 2
-FIRST = 192
-PRODUCTS = (((0, N), (N, FIRST), (FIRST, 2 * N), (2 * N, HALF)), tuple((j, j + N) for j in range(HALF, S, N)))
+FIRST = 224
+PRODUCTS = (((0, N), (N, 2 * N), (2 * N, HALF)), tuple((j, j + N) for j in range(HALF, S, N)))
 
 
 def tile_picked_kvput_tanh_p_kernel(tc, x_words, x_scales, mem, w1, offs, slot, out):
@@ -111,8 +111,11 @@ def tile_picked_kvput_tanh_p_kernel(tc, x_words, x_scales, mem, w1, offs, slot, 
                     start=True,
                     stop=True,
                 )
-                y = y_first[:, j0:j1] if j0 < FIRST else y_rest[:, j0 - FIRST : j1 - FIRST]
-                nc.scalar.activation(y, acc[:], TANH)
+                if j0 < FIRST:
+                    nc.scalar.activation(y_first[:, j0 : min(j1, FIRST)], acc[:, : min(j1, FIRST) - j0], TANH)
+                if j1 > FIRST:
+                    a = max(j0, FIRST)
+                    nc.scalar.activation(y_rest[:, a - FIRST : j1 - FIRST], acc[:, a - j0 :], TANH)
 
         nc.vector.tensor_tensor(window[:].indirect(entries(slot_sb, 0, FIRST)), y_first[:], zeros[:], mybir.AluOpType.add)
         nc.vector.tensor_copy(window[:].indirect(entries(slot_sb, FIRST, S)), y_rest[:])

@@ -13,6 +13,8 @@ U16 = mybir.dt.uint16
 U8 = mybir.dt.uint8
 FP8X4 = mybir.dt.float8_e4m3fn_x4
 TANH = mybir.ActivationFunctionType.Tanh
+COPY = mybir.ActivationFunctionType.Copy
+ALU = mybir.AluOpType
 
 P = 128
 PACK = 4
@@ -21,13 +23,19 @@ PLANE_ROWS = 4
 STRIPE = 16
 ALIGN = 64
 DMA_ALIGN = 256
+BANK = 512
 
 SPREAD_START, SPREAD_STEP = 32, 4
 SCALE_ROWS = 16
 
-HALF = S // 2
-FIRST = 224
-PRODUCTS = (((0, N), (N, 2 * N), (2 * N, HALF)), tuple((j, j + N) for j in range(HALF, S, N)))
+PIECES = ((0, 256), (256, 640), (640, 1024))
+PRODUCTS = (((0, 128), (128, 256)), ((256, 512), (512, 640)), ((640, 896), (896, 1024)))
+MEM_PIECES = 2
+MASK_VECTOR = 768
+STORES = (256, 512, 512, 512, 256)
+SCALES_AT = 3584
+CODES_AT = 4608
+OLD_AT = (0, 7168)
 
 
 def tile_picked_kvput_tanh_p_kernel(tc, x_words, x_scales, mem, w1, offs, slot, out):
@@ -35,12 +43,13 @@ def tile_picked_kvput_tanh_p_kernel(tc, x_words, x_scales, mem, w1, offs, slot, 
     with ExitStack() as ctx:
         keep = ctx.enter_context(tc.tile_pool(name="keep", bufs=1))
         reused = ctx.enter_context(tc.tile_pool(name="reused", bufs=1))
+        late = ctx.enter_context(tc.tile_pool(name="late", bufs=1))
         psum = ctx.enter_context(tc.psum_pool(name="psum", bufs=1))
 
         offs_sb = keep.tile([P, S // STRIPE], U16, name="offs_sb")
         slot_sb = keep.tile([P, S // STRIPE], U16, name="slot_sb")
         words = keep.tile([P, T], U32, name="words", align_bytes=DMA_ALIGN)
-        scales = keep.tile([P, T], U8, name="scales", align_bytes=DMA_ALIGN)
+        scales = reused.tile([P, T], U8, name="scales", align_bytes=DMA_ALIGN, offset=SCALES_AT)
         w_raw = keep.tile([P, PACK, N], F32, name="w_raw", align_bytes=DMA_ALIGN)
 
         scale_words = scales[:].bitcast(I32)
@@ -48,75 +57,91 @@ def tile_picked_kvput_tanh_p_kernel(tc, x_words, x_scales, mem, w1, offs, slot, 
         nc.vector.memset(scale_words[:, 209:416], 0)
         nc.gpsimd.memset(scale_words[:, 416:], 0)
 
+        nc.sync.dma_start(slot_sb[:], slot)
         nc.sync.dma_start(offs_sb[:], offs)
         nc.sync.dma_start(w_raw[:], w1.rearrange("(p j) m -> p j m", j=PACK))
         nc.sync.dma_start(scales[SPREAD_START : SPREAD_START + SPREAD_STEP * SCALE_ROWS : SPREAD_STEP, :].bitcast(I32), x_scales[0].bitcast(I32))
-        nc.sync.dma_start(
-            words[:].bitcast(I32),
-            x_words[0].rearrange("p n t -> p (n t)").bitcast(I32),
-        )
-
-        nc.sync.dma_start(slot_sb[:], slot)
-
-        w_grouped = reused.tile([P, N, PACK], BF16, name="w_grouped", align_bytes=ALIGN, offset=0)
-        w_codes = keep.tile([P, N], U32, name="w_codes", align_bytes=ALIGN)
-        w_plane = keep.tile([P, N], U8, name="w_plane", align_bytes=ALIGN)
-        nc.scalar.copy(out=w_grouped[:], in_=w_raw[:].rearrange("p j m -> p m j"))
-
-        x_plane = keep.tile([P, S], U8, name="x_plane", align_bytes=ALIGN)
-        nc.vector.memset(x_plane[:].bitcast(I32), 0)
-        zeros = keep.tile([P, FIRST], F32, name="zeros", align_bytes=ALIGN)
-        nc.vector.memset(zeros[:], 0.0)
+        nc.sync.dma_start(words[:].bitcast(I32), x_words[0].rearrange("p n t -> p (n t)").bitcast(I32))
 
         def entries(list_tile, j0, j1):
             return list_tile[:, j0 // STRIPE : j1 // STRIPE]
 
-        def pick_scales(h, spread):
-            j0, j1 = h * HALF, (h + 1) * HALF
-            nc.vector.tensor_copy(spread[:], scales[:].indirect(entries(offs_sb, j0, j1)))
-            for r in range(PLANE_ROWS):
-                nc.sync.dma_start(
-                    x_plane[r:P:QUADRANT, j0:j1].bitcast(I32),
-                    spread[
-                        SPREAD_START + SPREAD_STEP * r : SPREAD_START + SPREAD_STEP * SCALE_ROWS : SPREAD_STEP * PLANE_ROWS, :
-                    ].bitcast(I32),
-                )
+        longest = max(j1 - j0 for j0, j1 in PIECES)
+        mask = late.tile([P, U], I32, name="mask", align_bytes=ALIGN, offset=0)
+        ones = keep.tile([P, longest], F32, name="ones", align_bytes=ALIGN)
+        fresh = keep.tile([P, U], F32, name="fresh", align_bytes=ALIGN)
+        x_plane = keep.tile([P, S], U8, name="x_plane", align_bytes=ALIGN)
+        nc.vector.memset(fresh[:, : longest + 1], 0.0)
+        nc.vector.memset(fresh[:, longest + 1 : U // 2], 0.0)
+        nc.gpsimd.memset(fresh[:, U // 2 :], 0.0)
+        nc.scalar.activation(ones[:], fresh[:, :longest], COPY, bias=1.0)
+        nc.vector.memset(x_plane[:].bitcast(I32), 0)
 
-        spread_first = keep.tile([P, HALF], U8, name="spread_first", align_bytes=ALIGN)
-        pick_scales(0, spread_first)
-        nc.vector.quantize_mx(
-            out=w_codes[:].bitcast(FP8X4),
-            scales=w_plane[:],
-            in_=w_grouped[:].rearrange("p m j -> p (m j)"),
-        )
-        window = reused.tile([P, U], F32, name="window", align_bytes=DMA_ALIGN, offset=HALF)
-        spread_second = reused.tile([P, HALF], U8, name="spread_second", align_bytes=ALIGN, offset=0)
-        nc.sync.dma_start(window[:], mem)
-        pick_scales(1, spread_second)
+        w_grouped = late.tile([P, N, PACK], BF16, name="w_grouped", align_bytes=ALIGN, offset=0)
+        w_codes = reused.tile([P, N], U32, name="w_codes", align_bytes=ALIGN, offset=CODES_AT)
+        w_plane = keep.tile([P, N], U8, name="w_plane", align_bytes=ALIGN)
+        nc.vector.tensor_copy(w_grouped[:], w_raw[:].rearrange("p j m -> p m j"))
+        for j0, j1 in PIECES[:2]:
+            nc.scalar.activation(fresh[:].indirect(entries(slot_sb, j0, j1)), ones[:, : j1 - j0], COPY)
 
-        y_first = keep.tile([P, FIRST], F32, name="y_first", align_bytes=ALIGN)
-        y_rest = keep.tile([P, S - FIRST], F32, name="y_rest", align_bytes=ALIGN)
-        picked = keep.tile([P, S], U32, name="picked", align_bytes=ALIGN)
-        for h in range(S // HALF):
-            h0, h1 = h * HALF, (h + 1) * HALF
-            nc.vector.tensor_copy(picked[:, h0:h1], words[:].indirect(entries(offs_sb, h0, h1)))
-            for j0, j1 in PRODUCTS[h]:
-                acc = psum.tile([P, j1 - j0], F32, name="acc%d" % j0)
-                nc.tensor.matmul_mx(
-                    out=acc[:],
-                    lhsT=w_codes[:].bitcast(FP8X4),
-                    lhsT_scale=w_plane[:],
-                    rhs=picked[:, j0:j1].bitcast(FP8X4),
-                    rhs_scale=x_plane[:, j0:j1],
-                    start=True,
-                    stop=True,
-                )
-                if j0 < FIRST:
-                    nc.scalar.activation(y_first[:, j0 : min(j1, FIRST)], acc[:, : min(j1, FIRST) - j0], TANH)
-                if j1 > FIRST:
-                    a = max(j0, FIRST)
-                    nc.scalar.activation(y_rest[:, a - FIRST : j1 - FIRST], acc[:, a - j0 :], TANH)
+        spread = keep.tile([P, S], U8, name="spread", align_bytes=ALIGN)
+        nc.vector.tensor_copy(spread[:], scales[:].indirect(offs_sb[:]))
+        for r in range(PLANE_ROWS):
+            nc.sync.dma_start(
+                x_plane[r:P:QUADRANT, :].bitcast(I32),
+                spread[SPREAD_START + SPREAD_STEP * r : SPREAD_START + SPREAD_STEP * SCALE_ROWS : SPREAD_STEP * PLANE_ROWS, :].bitcast(I32),
+            )
+        nc.vector.quantize_mx(out=w_codes[:].bitcast(FP8X4), scales=w_plane[:], in_=w_grouped[:].rearrange("p m j -> p (m j)"))
+        nc.vector.tensor_scalar(mask[:, :MASK_VECTOR], fresh[:, :MASK_VECTOR], 0.0, -1.0, ALU.is_equal, ALU.mult)
+        nc.scalar.activation(mask[:, MASK_VECTOR:].bitcast(U32), fresh[:, MASK_VECTOR:], COPY, bias=2.0**32, scale=-(2.0**32))
 
-        nc.vector.tensor_tensor(window[:].indirect(entries(slot_sb, 0, FIRST)), y_first[:], zeros[:], mybir.AluOpType.add)
-        nc.vector.tensor_copy(window[:].indirect(entries(slot_sb, FIRST, S)), y_rest[:])
-        nc.sync.dma_start(out, window[:])
+        width = U // MEM_PIECES
+        olds = []
+        for c in range(MEM_PIECES):
+            old = reused.tile([P, width], F32, name="old%d" % c, align_bytes=DMA_ALIGN, offset=OLD_AT[c])
+            nc.sync.dma_start(old[:], mem[:, c * width : (c + 1) * width])
+            olds.append(old)
+
+        def product(acc, picked, h0, a0, j0, j1):
+            nc.tensor.matmul_mx(
+                out=acc[:, j0 - a0 : j1 - a0],
+                lhsT=w_codes[:].bitcast(FP8X4),
+                lhsT_scale=w_plane[:],
+                rhs=picked[:, j0 - h0 : j1 - h0].bitcast(FP8X4),
+                rhs_scale=x_plane[:, j0:j1],
+                start=True,
+                stop=True,
+            )
+
+        ys = []
+        for i, (h0, h1) in enumerate(PIECES):
+            picked = keep.tile([P, h1 - h0], U32, name="picked%d" % i, align_bytes=ALIGN)
+            nc.vector.tensor_copy(picked[:], words[:].indirect(entries(offs_sb, h0, h1)))
+            y = keep.tile([P, h1 - h0], F32, name="y%d" % i, align_bytes=ALIGN)
+            ys.append(y)
+            if i == 0:
+                for b, (j0, j1) in enumerate(PRODUCTS[0]):
+                    acc = psum.tile([P, BANK], F32, name="acc%d" % b)
+                    product(acc, picked, h0, j0, j0, j1)
+                    nc.scalar.activation(y[:, j0:j1], acc[:, : j1 - j0], TANH)
+                nc.scalar.activation(fresh[:].indirect(entries(slot_sb, h0, h1)), y[:], COPY)
+            else:
+                acc = psum.tile([P, BANK], F32, name="acc%d" % (i - 1))
+                for j0, j1 in PRODUCTS[i]:
+                    product(acc, picked, h0, h0, j0, j1)
+                nc.scalar.activation(y[:], acc[:, : h1 - h0], TANH)
+        nc.scalar.activation(fresh[:].indirect(entries(slot_sb, *PIECES[1])), ys[1][:], COPY)
+
+        kept = keep.tile([P, U], F32, name="kept", align_bytes=ALIGN)
+        for c in range(MEM_PIECES):
+            cols = slice(c * width, (c + 1) * width)
+            nc.vector.tensor_tensor(kept[:, cols].bitcast(I32), olds[c][:].bitcast(I32), mask[:, cols], ALU.bitwise_and)
+        nc.vector.tensor_copy(kept[:].indirect(entries(slot_sb, *PIECES[2])), ys[2][:])
+
+        c0 = 0
+        for c, step in enumerate(STORES):
+            cols = slice(c0, c0 + step)
+            c0 = c0 + step
+            merged = keep.tile([P, step], F32, name="merged%d" % c, align_bytes=DMA_ALIGN)
+            nc.vector.tensor_tensor(merged[:], kept[:, cols], fresh[:, cols], ALU.add)
+            nc.sync.dma_start(out[:, cols], merged[:])

@@ -28,14 +28,17 @@ BANK = 512
 SPREAD_START, SPREAD_STEP = 32, 4
 SCALE_ROWS = 16
 
-PIECES = ((0, 256), (256, 640), (640, 1024))
-PRODUCTS = (((0, 128), (128, 256)), ((256, 512), (512, 640)), ((640, 896), (896, 1024)))
+FIRST = 256
+LAST = 320
+SCALAR_PIECES = ((0, FIRST), (S - LAST, S))
+GATHERS = ((0, 256), (256, 768), (768, 1024))
+BANKS = (((0, 128),), ((128, 256),), ((256, 768),), ((768, 1024),))
 MEM_PIECES = 2
 MASK_VECTOR = 768
 STORES = (256, 512, 512, 512, 256)
-SCALES_AT = 3584
-CODES_AT = 4608
-OLD_AT = (0, 7168)
+GROUPED_AT = 3840
+SPREAD_AT = 4096
+OLD_AT = (0, 4608)
 
 
 def tile_picked_kvput_tanh_p_kernel(tc, x_words, x_scales, mem, w1, offs, slot, out):
@@ -49,7 +52,7 @@ def tile_picked_kvput_tanh_p_kernel(tc, x_words, x_scales, mem, w1, offs, slot, 
         offs_sb = keep.tile([P, S // STRIPE], U16, name="offs_sb")
         slot_sb = keep.tile([P, S // STRIPE], U16, name="slot_sb")
         words = keep.tile([P, T], U32, name="words", align_bytes=DMA_ALIGN)
-        scales = reused.tile([P, T], U8, name="scales", align_bytes=DMA_ALIGN, offset=SCALES_AT)
+        scales = reused.tile([P, T], U8, name="scales", align_bytes=DMA_ALIGN, offset=0)
         w_raw = keep.tile([P, PACK, N], F32, name="w_raw", align_bytes=DMA_ALIGN)
 
         scale_words = scales[:].bitcast(I32)
@@ -66,8 +69,8 @@ def tile_picked_kvput_tanh_p_kernel(tc, x_words, x_scales, mem, w1, offs, slot, 
         def entries(list_tile, j0, j1):
             return list_tile[:, j0 // STRIPE : j1 // STRIPE]
 
-        longest = max(j1 - j0 for j0, j1 in PIECES)
-        mask = late.tile([P, U], I32, name="mask", align_bytes=ALIGN, offset=0)
+        longest = max(j1 - j0 for j0, j1 in SCALAR_PIECES)
+        mask = reused.tile([P, U], I32, name="mask", align_bytes=ALIGN, offset=0)
         ones = keep.tile([P, longest], F32, name="ones", align_bytes=ALIGN)
         fresh = keep.tile([P, U], F32, name="fresh", align_bytes=ALIGN)
         x_plane = keep.tile([P, S], U8, name="x_plane", align_bytes=ALIGN)
@@ -77,66 +80,67 @@ def tile_picked_kvput_tanh_p_kernel(tc, x_words, x_scales, mem, w1, offs, slot, 
         nc.scalar.activation(ones[:], fresh[:, :longest], COPY, bias=1.0)
         nc.vector.memset(x_plane[:].bitcast(I32), 0)
 
-        w_grouped = late.tile([P, N, PACK], BF16, name="w_grouped", align_bytes=ALIGN, offset=0)
-        w_codes = reused.tile([P, N], U32, name="w_codes", align_bytes=ALIGN, offset=CODES_AT)
+        w_grouped = late.tile([P, N, PACK], BF16, name="w_grouped", align_bytes=ALIGN, offset=GROUPED_AT)
+        w_codes = keep.tile([P, N], U32, name="w_codes", align_bytes=ALIGN)
         w_plane = keep.tile([P, N], U8, name="w_plane", align_bytes=ALIGN)
         nc.vector.tensor_copy(w_grouped[:], w_raw[:].rearrange("p j m -> p m j"))
-        for j0, j1 in PIECES[:2]:
+        for j0, j1 in SCALAR_PIECES:
             nc.scalar.activation(fresh[:].indirect(entries(slot_sb, j0, j1)), ones[:, : j1 - j0], COPY)
 
-        spread = keep.tile([P, S], U8, name="spread", align_bytes=ALIGN)
-        nc.vector.tensor_copy(spread[:], scales[:].indirect(offs_sb[:]))
-        for r in range(PLANE_ROWS):
-            nc.sync.dma_start(
-                x_plane[r:P:QUADRANT, :].bitcast(I32),
-                spread[SPREAD_START + SPREAD_STEP * r : SPREAD_START + SPREAD_STEP * SCALE_ROWS : SPREAD_STEP * PLANE_ROWS, :].bitcast(I32),
-            )
+        def pick_scales(spread, g0, g1, j0):
+            nc.vector.tensor_copy(spread[:], scales[:].indirect(entries(offs_sb, g0, g1)))
+            for r in range(PLANE_ROWS):
+                nc.sync.dma_start(
+                    x_plane[r:P:QUADRANT, j0:g1].bitcast(I32),
+                    spread[SPREAD_START + SPREAD_STEP * r : SPREAD_START + SPREAD_STEP * SCALE_ROWS : SPREAD_STEP * PLANE_ROWS, j0 - g0 :].bitcast(I32),
+                )
+
+        cut = S // 2
+        spread_first = keep.tile([P, cut], U8, name="spread_first", align_bytes=ALIGN)
+        pick_scales(spread_first, 0, cut, 0)
         nc.vector.quantize_mx(out=w_codes[:].bitcast(FP8X4), scales=w_plane[:], in_=w_grouped[:].rearrange("p m j -> p (m j)"))
-        nc.vector.tensor_scalar(mask[:, :MASK_VECTOR], fresh[:, :MASK_VECTOR], 0.0, -1.0, ALU.is_equal, ALU.mult)
-        nc.scalar.activation(mask[:, MASK_VECTOR:].bitcast(U32), fresh[:, MASK_VECTOR:], COPY, bias=2.0**32, scale=-(2.0**32))
 
         width = U // MEM_PIECES
         olds = []
         for c in range(MEM_PIECES):
-            old = reused.tile([P, width], F32, name="old%d" % c, align_bytes=DMA_ALIGN, offset=OLD_AT[c])
+            old = late.tile([P, width], F32, name="old%d" % c, align_bytes=DMA_ALIGN, offset=OLD_AT[c])
             nc.sync.dma_start(old[:], mem[:, c * width : (c + 1) * width])
             olds.append(old)
+        spread_second = late.tile([P, S // 2], U8, name="spread_second", align_bytes=ALIGN, offset=SPREAD_AT)
+        pick_scales(spread_second, S // 2, S, cut)
+        nc.vector.tensor_scalar(mask[:, :MASK_VECTOR], fresh[:, :MASK_VECTOR], 0.0, -1.0, ALU.is_equal, ALU.mult)
+        nc.scalar.activation(mask[:, MASK_VECTOR:].bitcast(U32), fresh[:, MASK_VECTOR:], COPY, bias=2.0**32, scale=-(2.0**32))
 
-        def product(acc, picked, h0, a0, j0, j1):
-            nc.tensor.matmul_mx(
-                out=acc[:, j0 - a0 : j1 - a0],
-                lhsT=w_codes[:].bitcast(FP8X4),
-                lhsT_scale=w_plane[:],
-                rhs=picked[:, j0 - h0 : j1 - h0].bitcast(FP8X4),
-                rhs_scale=x_plane[:, j0:j1],
-                start=True,
-                stop=True,
-            )
+        picked = keep.tile([P, S], U32, name="picked", align_bytes=ALIGN)
+        for g0, g1 in GATHERS:
+            nc.vector.tensor_copy(picked[:, g0:g1], words[:].indirect(entries(offs_sb, g0, g1)))
 
-        ys = []
-        for i, (h0, h1) in enumerate(PIECES):
-            picked = keep.tile([P, h1 - h0], U32, name="picked%d" % i, align_bytes=ALIGN)
-            nc.vector.tensor_copy(picked[:], words[:].indirect(entries(offs_sb, h0, h1)))
-            y = keep.tile([P, h1 - h0], F32, name="y%d" % i, align_bytes=ALIGN)
-            ys.append(y)
-            if i == 0:
-                for b, (j0, j1) in enumerate(PRODUCTS[0]):
-                    acc = psum.tile([P, BANK], F32, name="acc%d" % b)
-                    product(acc, picked, h0, j0, j0, j1)
-                    nc.scalar.activation(y[:, j0:j1], acc[:, : j1 - j0], TANH)
-                nc.scalar.activation(fresh[:].indirect(entries(slot_sb, h0, h1)), y[:], COPY)
-            else:
-                acc = psum.tile([P, BANK], F32, name="acc%d" % (i - 1))
-                for j0, j1 in PRODUCTS[i]:
-                    product(acc, picked, h0, h0, j0, j1)
-                nc.scalar.activation(y[:], acc[:, : h1 - h0], TANH)
-        nc.scalar.activation(fresh[:].indirect(entries(slot_sb, *PIECES[1])), ys[1][:], COPY)
+        y_first = keep.tile([P, FIRST], F32, name="y_first", align_bytes=ALIGN)
+        y_rest = keep.tile([P, S - FIRST], F32, name="y_rest", align_bytes=ALIGN)
+        for b, products in enumerate(BANKS):
+            a0, a1 = products[0][0], products[-1][1]
+            acc = psum.tile([P, BANK], F32, name="acc%d" % (b % 2))
+            for j0, j1 in products:
+                nc.tensor.matmul_mx(
+                    out=acc[:, j0 - a0 : j1 - a0],
+                    lhsT=w_codes[:].bitcast(FP8X4),
+                    lhsT_scale=w_plane[:],
+                    rhs=picked[:, j0:j1].bitcast(FP8X4),
+                    rhs_scale=x_plane[:, j0:j1],
+                    start=True,
+                    stop=True,
+                )
+            y = y_first[:, a0:a1] if a1 <= FIRST else y_rest[:, a0 - FIRST : a1 - FIRST]
+            nc.scalar.activation(y, acc[:, : a1 - a0], TANH)
+            if a1 == FIRST:
+                nc.scalar.activation(fresh[:].indirect(entries(slot_sb, 0, FIRST)), y_first[:], COPY)
+        nc.scalar.activation(fresh[:].indirect(entries(slot_sb, S - LAST, S)), y_rest[:, S - LAST - FIRST :], COPY)
 
         kept = keep.tile([P, U], F32, name="kept", align_bytes=ALIGN)
         for c in range(MEM_PIECES):
             cols = slice(c * width, (c + 1) * width)
             nc.vector.tensor_tensor(kept[:, cols].bitcast(I32), olds[c][:].bitcast(I32), mask[:, cols], ALU.bitwise_and)
-        nc.vector.tensor_copy(kept[:].indirect(entries(slot_sb, *PIECES[2])), ys[2][:])
+        nc.vector.tensor_copy(kept[:].indirect(entries(slot_sb, FIRST, S - LAST)), y_rest[:, : S - LAST - FIRST])
 
         c0 = 0
         for c, step in enumerate(STORES):

@@ -28,17 +28,15 @@ BANK = 512
 SPREAD_START, SPREAD_STEP = 32, 4
 SCALE_ROWS = 16
 
+FLT_MAX = (2.0 - 2.0**-23) * 2.0**127
 FIRST = 256
 LAST = 320
 SCALAR_PIECES = ((0, FIRST), (S - LAST, S))
 GATHERS = ((0, 256), (256, 768), (768, 1024))
 BANKS = (((0, 128),), ((128, 256),), ((256, 768),), ((768, 1024),))
-MEM_PIECES = 2
-MASK_VECTOR = 768
-STORES = (256, 512, 512, 512, 256)
-GROUPED_AT = 3840
-SPREAD_AT = 4096
-OLD_AT = (0, 4608)
+CAP_VECTOR = 768
+TAIL = (("min", 0, 1280), ("scatter", FIRST, S - LAST), ("max", 0, 256), ("max", 256, 768), ("min", 1280, 1664), ("max", 768, 1280), ("min", 1664, 2048), ("max", 1280, 1664), ("max", 1664, 2048))
+HALF = S // 2
 
 
 def tile_picked_kvput_tanh_p_kernel(tc, x_words, x_scales, mem, w1, offs, slot, out):
@@ -69,47 +67,43 @@ def tile_picked_kvput_tanh_p_kernel(tc, x_words, x_scales, mem, w1, offs, slot, 
         def entries(list_tile, j0, j1):
             return list_tile[:, j0 // STRIPE : j1 // STRIPE]
 
-        longest = max(j1 - j0 for j0, j1 in SCALAR_PIECES)
-        mask = reused.tile([P, U], I32, name="mask", align_bytes=ALIGN, offset=0)
-        ones = keep.tile([P, longest], F32, name="ones", align_bytes=ALIGN)
+        longest = max(FIRST, LAST)
+        cap = reused.tile([P, U], F32, name="cap", align_bytes=ALIGN, offset=0)
+        twos = keep.tile([P, longest], F32, name="twos", align_bytes=ALIGN)
         fresh = keep.tile([P, U], F32, name="fresh", align_bytes=ALIGN)
         x_plane = keep.tile([P, S], U8, name="x_plane", align_bytes=ALIGN)
-        nc.vector.memset(fresh[:, : longest + 1], 0.0)
-        nc.vector.memset(fresh[:, longest + 1 : U // 2], 0.0)
-        nc.gpsimd.memset(fresh[:, U // 2 :], 0.0)
-        nc.scalar.activation(ones[:], fresh[:, :longest], COPY, bias=1.0)
+        nc.vector.memset(fresh[:, : longest + 1], -FLT_MAX)
+        nc.vector.memset(fresh[:, longest + 1 : U // 2], -FLT_MAX)
+        nc.gpsimd.memset(fresh[:, U // 2 :], -FLT_MAX)
+        nc.scalar.activation(twos[:], fresh[:, :longest], COPY, bias=2.0, scale=0.0)
         nc.vector.memset(x_plane[:].bitcast(I32), 0)
 
-        w_grouped = late.tile([P, N, PACK], BF16, name="w_grouped", align_bytes=ALIGN, offset=GROUPED_AT)
+        w_grouped = late.tile([P, N, PACK], BF16, name="w_grouped", align_bytes=ALIGN, offset=0)
         w_codes = keep.tile([P, N], U32, name="w_codes", align_bytes=ALIGN)
         w_plane = keep.tile([P, N], U8, name="w_plane", align_bytes=ALIGN)
         nc.vector.tensor_copy(w_grouped[:], w_raw[:].rearrange("p j m -> p m j"))
         for j0, j1 in SCALAR_PIECES:
-            nc.scalar.activation(fresh[:].indirect(entries(slot_sb, j0, j1)), ones[:, : j1 - j0], COPY)
+            nc.scalar.activation(fresh[:].indirect(entries(slot_sb, j0, j1)), twos[:, : j1 - j0], COPY)
 
-        def pick_scales(spread, g0, g1, j0):
-            nc.vector.tensor_copy(spread[:], scales[:].indirect(entries(offs_sb, g0, g1)))
+        def pick_scales(h, spread):
+            j0, j1 = h * HALF, (h + 1) * HALF
+            nc.vector.tensor_copy(spread[:], scales[:].indirect(entries(offs_sb, j0, j1)))
             for r in range(PLANE_ROWS):
                 nc.sync.dma_start(
-                    x_plane[r:P:QUADRANT, j0:g1].bitcast(I32),
-                    spread[SPREAD_START + SPREAD_STEP * r : SPREAD_START + SPREAD_STEP * SCALE_ROWS : SPREAD_STEP * PLANE_ROWS, j0 - g0 :].bitcast(I32),
+                    x_plane[r:P:QUADRANT, j0:j1].bitcast(I32),
+                    spread[SPREAD_START + SPREAD_STEP * r : SPREAD_START + SPREAD_STEP * SCALE_ROWS : SPREAD_STEP * PLANE_ROWS, :].bitcast(I32),
                 )
 
-        cut = S // 2
-        spread_first = keep.tile([P, cut], U8, name="spread_first", align_bytes=ALIGN)
-        pick_scales(spread_first, 0, cut, 0)
+        spread_first = keep.tile([P, HALF], U8, name="spread_first", align_bytes=ALIGN)
+        pick_scales(0, spread_first)
         nc.vector.quantize_mx(out=w_codes[:].bitcast(FP8X4), scales=w_plane[:], in_=w_grouped[:].rearrange("p m j -> p (m j)"))
 
-        width = U // MEM_PIECES
-        olds = []
-        for c in range(MEM_PIECES):
-            old = late.tile([P, width], F32, name="old%d" % c, align_bytes=DMA_ALIGN, offset=OLD_AT[c])
-            nc.sync.dma_start(old[:], mem[:, c * width : (c + 1) * width])
-            olds.append(old)
-        spread_second = late.tile([P, S // 2], U8, name="spread_second", align_bytes=ALIGN, offset=SPREAD_AT)
-        pick_scales(spread_second, S // 2, S, cut)
-        nc.vector.tensor_scalar(mask[:, :MASK_VECTOR], fresh[:, :MASK_VECTOR], 0.0, -1.0, ALU.is_equal, ALU.mult)
-        nc.scalar.activation(mask[:, MASK_VECTOR:].bitcast(U32), fresh[:, MASK_VECTOR:], COPY, bias=2.0**32, scale=-(2.0**32))
+        window = late.tile([P, U], F32, name="window", align_bytes=DMA_ALIGN, offset=HALF)
+        spread_second = late.tile([P, HALF], U8, name="spread_second", align_bytes=ALIGN, offset=0)
+        nc.sync.dma_start(window[:], mem)
+        pick_scales(1, spread_second)
+        nc.vector.tensor_scalar(cap[:, :CAP_VECTOR], fresh[:, :CAP_VECTOR], -1.0, None, ALU.mult)
+        nc.scalar.activation(cap[:, CAP_VECTOR:], fresh[:, CAP_VECTOR:], COPY, scale=-1.0)
 
         picked = keep.tile([P, S], U32, name="picked", align_bytes=ALIGN)
         for g0, g1 in GATHERS:
@@ -136,16 +130,12 @@ def tile_picked_kvput_tanh_p_kernel(tc, x_words, x_scales, mem, w1, offs, slot, 
                 nc.scalar.activation(fresh[:].indirect(entries(slot_sb, 0, FIRST)), y_first[:], COPY)
         nc.scalar.activation(fresh[:].indirect(entries(slot_sb, S - LAST, S)), y_rest[:, S - LAST - FIRST :], COPY)
 
-        kept = keep.tile([P, U], F32, name="kept", align_bytes=ALIGN)
-        for c in range(MEM_PIECES):
-            cols = slice(c * width, (c + 1) * width)
-            nc.vector.tensor_tensor(kept[:, cols].bitcast(I32), olds[c][:].bitcast(I32), mask[:, cols], ALU.bitwise_and)
-        nc.vector.tensor_copy(kept[:].indirect(entries(slot_sb, FIRST, S - LAST)), y_rest[:, : S - LAST - FIRST])
-
-        c0 = 0
-        for c, step in enumerate(STORES):
-            cols = slice(c0, c0 + step)
-            c0 = c0 + step
-            merged = keep.tile([P, step], F32, name="merged%d" % c, align_bytes=DMA_ALIGN)
-            nc.vector.tensor_tensor(merged[:], kept[:, cols], fresh[:, cols], ALU.add)
-            nc.sync.dma_start(out[:, cols], merged[:])
+        merged = keep.tile([P, U], F32, name="merged", align_bytes=DMA_ALIGN)
+        for kind, c0, c1 in TAIL:
+            if kind == "min":
+                nc.vector.tensor_tensor(window[:, c0:c1], window[:, c0:c1], cap[:, c0:c1], ALU.min)
+            elif kind == "scatter":
+                nc.vector.tensor_copy(window[:].indirect(entries(slot_sb, c0, c1)), y_rest[:, c0 - FIRST : c1 - FIRST])
+            else:
+                nc.vector.tensor_tensor(merged[:, c0:c1], window[:, c0:c1], fresh[:, c0:c1], ALU.max)
+                nc.sync.dma_start(out[:, c0:c1], merged[:, c0:c1])

@@ -34,8 +34,8 @@ LAST = 320
 SCALAR_PIECES = ((0, FIRST), (S - LAST, S))
 GATHERS = ((0, 256), (256, 768), (768, 1024))
 BANKS = (((0, 128),), ((128, 256),), ((256, 768),), ((768, 1024),))
-CAP_VECTOR = 768
-TAIL = (("min", 0, 1280), ("scatter", FIRST, S - LAST), ("max", 0, 256), ("max", 256, 768), ("min", 1280, 1664), ("max", 768, 1280), ("min", 1664, 2048), ("max", 1280, 1664), ("max", 1664, 2048))
+CAP_VECTOR = 1024
+TAIL = (("min", 0, 1792), ("scatter", FIRST, S - LAST), ("max", 0, 256), ("min", 1792, 2048), ("max", 256, 768), ("max", 768, 1280), ("max", 1280, 1792), ("max", 1792, 2048))
 HALF = S // 2
 
 
@@ -102,7 +102,7 @@ def tile_picked_kvput_tanh_p_kernel(tc, x_words, x_scales, mem, w1, offs, slot, 
         spread_second = late.tile([P, HALF], U8, name="spread_second", align_bytes=ALIGN, offset=0)
         nc.sync.dma_start(window[:], mem)
         pick_scales(1, spread_second)
-        nc.vector.tensor_scalar(cap[:, :CAP_VECTOR], fresh[:, :CAP_VECTOR], -1.0, None, ALU.mult)
+        nc.gpsimd.tensor_scalar(cap[:, :CAP_VECTOR], fresh[:, :CAP_VECTOR], -1.0, 0.0, ALU.mult, ALU.add)
         nc.scalar.activation(cap[:, CAP_VECTOR:], fresh[:, CAP_VECTOR:], COPY, scale=-1.0)
 
         picked = keep.tile([P, S], U32, name="picked", align_bytes=ALIGN)

@@ -30,11 +30,11 @@ SCALE_ROWS = 16
 
 FLT_MAX = (2.0 - 2.0**-23) * 2.0**127
 FIRST = 256
-LAST = 320
+LAST = 384
 SCALAR_PIECES = ((0, FIRST), (S - LAST, S))
-GATHERS = ((0, 256), (256, 768), (768, 1024))
+GATHERS = ((0, 256), (256, 1024))
 BANKS = (((0, 128),), ((128, 256),), ((256, 768),), ((768, 1024),))
-CAP_VECTOR = 1024
+CAP_VECTOR = 1088
 TAIL = (("min", 0, 1792), ("scatter", FIRST, S - LAST), ("max", 0, 256), ("min", 1792, 2048), ("max", 256, 768), ("max", 768, 1280), ("max", 1280, 1792), ("max", 1792, 2048))
 HALF = S // 2
 
@@ -59,8 +59,8 @@ def tile_picked_kvput_tanh_p_kernel(tc, x_words, x_scales, mem, w1, offs, slot, 
         nc.gpsimd.memset(scale_words[:, 416:], 0)
 
         nc.sync.dma_start(slot_sb[:], slot)
-        nc.sync.dma_start(offs_sb[:], offs)
         nc.sync.dma_start(w_raw[:], w1.rearrange("(p j) m -> p j m", j=PACK))
+        nc.sync.dma_start(offs_sb[:], offs)
         nc.sync.dma_start(scales[SPREAD_START : SPREAD_START + SPREAD_STEP * SCALE_ROWS : SPREAD_STEP, :].bitcast(I32), x_scales[0].bitcast(I32))
         nc.sync.dma_start(words[:].bitcast(I32), x_words[0].rearrange("p n t -> p (n t)").bitcast(I32))
 

@@ -31,11 +31,11 @@ SCALE_ROWS = 16
 FLT_MAX = (2.0 - 2.0**-23) * 2.0**127
 FIRST = 256
 LAST = 384
-SCALAR_PIECES = ((0, FIRST), (S - LAST, S))
+SCALAR_PIECES = ((0, FIRST), (FIRST, FIRST + LAST))
 GATHERS = ((0, 256), (256, 1024))
-BANKS = (((0, 128),), ((128, 256),), ((256, 768),), ((768, 1024),))
+BANKS = (((0, 128),), ((128, 256),), ((256, 512), (512, 640)), ((640, 896), (896, 1024)))
 CAP_VECTOR = 1088
-TAIL = (("min", 0, 1792), ("scatter", FIRST, S - LAST), ("max", 0, 256), ("min", 1792, 2048), ("max", 256, 768), ("max", 768, 1280), ("max", 1280, 1792), ("max", 1792, 2048))
+TAIL = (("min", 0, 2048), ("scatter", FIRST + LAST, S), ("max", 0, 448), ("max", 448, 896), ("max", 896, 1280), ("max", 1280, 1664), ("max", 1664, 2048))
 HALF = S // 2
 
 
@@ -128,7 +128,7 @@ def tile_picked_kvput_tanh_p_kernel(tc, x_words, x_scales, mem, w1, offs, slot, 
             nc.scalar.activation(y, acc[:, : a1 - a0], TANH)
             if a1 == FIRST:
                 nc.scalar.activation(fresh[:].indirect(entries(slot_sb, 0, FIRST)), y_first[:], COPY)
-        nc.scalar.activation(fresh[:].indirect(entries(slot_sb, S - LAST, S)), y_rest[:, S - LAST - FIRST :], COPY)
+        nc.scalar.activation(fresh[:].indirect(entries(slot_sb, FIRST, FIRST + LAST)), y_rest[:, :LAST], COPY)
 
         merged = keep.tile([P, U], F32, name="merged", align_bytes=DMA_ALIGN)
         for kind, c0, c1 in TAIL:

@@ -21,97 +21,104 @@ PACK = 4
 QUADRANT = 32
 PLANE_ROWS = 4
 STRIPE = 16
+BANK = 512
 ALIGN = 64
 DMA_ALIGN = 256
-BANK = 512
+FLT_MAX = (2.0 - 2.0**-23) * 2.0**127
+MARK = 2.0
 
 SPREAD_START, SPREAD_STEP = 32, 4
 SCALE_ROWS = 16
+CLEAR_CUT, CLEAR_VECTOR = 209, 416
+FILL_CUT, FILL_VECTOR = 463, 928
+MARKS_SCALAR = 15
 
-FLT_MAX = (2.0 - 2.0**-23) * 2.0**127
-FIRST = 256
-LAST = 384
-SCALAR_PIECES = ((0, FIRST), (FIRST, FIRST + LAST))
-GATHERS = ((0, 256), (256, 1024))
-BANKS = (((0, 128),), ((128, 256),), ((256, 512), (512, 640)), ((640, 896), (896, 1024)))
-CAP_VECTOR = 1088
-TAIL = (("min", 0, 2048), ("scatter", FIRST + LAST, S), ("max", 0, 448), ("max", 448, 896), ("max", 896, 1280), ("max", 1280, 1664), ("max", 1664, 2048))
+FIRST, SCALAR_END = 256, 640
+PIECES = ((0, FIRST), (FIRST, SCALAR_END), (SCALAR_END, S))
 HALF = S // 2
+FILLINGS = (((0, 128),), ((128, 256),), ((256, 512), (512, 640)), ((640, 896), (896, 1024)))
+CAP_GPSIMD = 1088
+MEM_PIECES = 1
+STORES = (448, 448, 384, 384, 384)
 
 
 def tile_picked_kvput_tanh_p_kernel(tc, x_words, x_scales, mem, w1, offs, slot, out):
     nc = tc.nc
     with ExitStack() as ctx:
         keep = ctx.enter_context(tc.tile_pool(name="keep", bufs=1))
-        reused = ctx.enter_context(tc.tile_pool(name="reused", bufs=1))
-        late = ctx.enter_context(tc.tile_pool(name="late", bufs=1))
+        after_scales = ctx.enter_context(tc.tile_pool(name="after_scales", bufs=1))
+        after_weights = ctx.enter_context(tc.tile_pool(name="after_weights", bufs=1))
         psum = ctx.enter_context(tc.psum_pool(name="psum", bufs=1))
 
         offs_sb = keep.tile([P, S // STRIPE], U16, name="offs_sb")
         slot_sb = keep.tile([P, S // STRIPE], U16, name="slot_sb")
         words = keep.tile([P, T], U32, name="words", align_bytes=DMA_ALIGN)
-        scales = reused.tile([P, T], U8, name="scales", align_bytes=DMA_ALIGN, offset=0)
+        scales = after_scales.tile([P, T], U8, name="scales", align_bytes=DMA_ALIGN, offset=0)
         w_raw = keep.tile([P, PACK, N], F32, name="w_raw", align_bytes=DMA_ALIGN)
 
         scale_words = scales[:].bitcast(I32)
-        nc.vector.memset(scale_words[:, :209], 0)
-        nc.vector.memset(scale_words[:, 209:416], 0)
-        nc.gpsimd.memset(scale_words[:, 416:], 0)
+        nc.vector.memset(scale_words[:, :CLEAR_CUT], 0)
+        nc.vector.memset(scale_words[:, CLEAR_CUT:CLEAR_VECTOR], 0)
+        nc.gpsimd.memset(scale_words[:, CLEAR_VECTOR:], 0)
 
         nc.sync.dma_start(slot_sb[:], slot)
         nc.sync.dma_start(w_raw[:], w1.rearrange("(p j) m -> p j m", j=PACK))
         nc.sync.dma_start(offs_sb[:], offs)
-        nc.sync.dma_start(scales[SPREAD_START : SPREAD_START + SPREAD_STEP * SCALE_ROWS : SPREAD_STEP, :].bitcast(I32), x_scales[0].bitcast(I32))
+        spread_end = SPREAD_START + SPREAD_STEP * SCALE_ROWS
+        nc.sync.dma_start(scales[SPREAD_START:spread_end:SPREAD_STEP, :].bitcast(I32), x_scales[0].bitcast(I32))
         nc.sync.dma_start(words[:].bitcast(I32), x_words[0].rearrange("p n t -> p (n t)").bitcast(I32))
 
         def entries(list_tile, j0, j1):
             return list_tile[:, j0 // STRIPE : j1 // STRIPE]
 
-        longest = max(FIRST, LAST)
-        cap = reused.tile([P, U], F32, name="cap", align_bytes=ALIGN, offset=0)
-        twos = keep.tile([P, longest], F32, name="twos", align_bytes=ALIGN)
+        longest = SCALAR_END - FIRST
+        cap = after_scales.tile([P, U], F32, name="cap", align_bytes=ALIGN, offset=0)
+        marks = keep.tile([P, longest], F32, name="marks", align_bytes=ALIGN)
         fresh = keep.tile([P, U], F32, name="fresh", align_bytes=ALIGN)
         x_plane = keep.tile([P, S], U8, name="x_plane", align_bytes=ALIGN)
-        nc.vector.memset(fresh[:, : longest + 1], -FLT_MAX)
-        nc.vector.memset(fresh[:, longest + 1 : U // 2], -FLT_MAX)
-        nc.gpsimd.memset(fresh[:, U // 2 :], -FLT_MAX)
-        nc.scalar.activation(twos[:], fresh[:, :longest], COPY, bias=2.0, scale=0.0)
+        nc.vector.memset(marks[:, MARKS_SCALAR:], MARK)
+        nc.scalar.activation(marks[:, :MARKS_SCALAR], marks[:, MARKS_SCALAR : 2 * MARKS_SCALAR], COPY)
+        nc.vector.memset(fresh[:, :FILL_CUT], -FLT_MAX)
+        nc.vector.memset(fresh[:, FILL_CUT:FILL_VECTOR], -FLT_MAX)
+        nc.gpsimd.memset(fresh[:, FILL_VECTOR:], -FLT_MAX)
         nc.vector.memset(x_plane[:].bitcast(I32), 0)
 
-        w_grouped = late.tile([P, N, PACK], BF16, name="w_grouped", align_bytes=ALIGN, offset=0)
+        w_grouped = after_weights.tile([P, N, PACK], BF16, name="w_grouped", align_bytes=ALIGN, offset=0)
         w_codes = keep.tile([P, N], U32, name="w_codes", align_bytes=ALIGN)
         w_plane = keep.tile([P, N], U8, name="w_plane", align_bytes=ALIGN)
         nc.vector.tensor_copy(w_grouped[:], w_raw[:].rearrange("p j m -> p m j"))
-        for j0, j1 in SCALAR_PIECES:
-            nc.scalar.activation(fresh[:].indirect(entries(slot_sb, j0, j1)), twos[:, : j1 - j0], COPY)
+        for j0, j1 in PIECES[:2]:
+            nc.scalar.activation(fresh[:].indirect(entries(slot_sb, j0, j1)), marks[:, : j1 - j0], COPY)
 
-        def pick_scales(h, spread):
-            j0, j1 = h * HALF, (h + 1) * HALF
-            nc.vector.tensor_copy(spread[:], scales[:].indirect(entries(offs_sb, j0, j1)))
+        def pick_scales(spread, g0, g1, j0):
+            nc.vector.tensor_copy(spread[:], scales[:].indirect(entries(offs_sb, g0, g1)))
             for r in range(PLANE_ROWS):
-                nc.sync.dma_start(
-                    x_plane[r:P:QUADRANT, j0:j1].bitcast(I32),
-                    spread[SPREAD_START + SPREAD_STEP * r : SPREAD_START + SPREAD_STEP * SCALE_ROWS : SPREAD_STEP * PLANE_ROWS, :].bitcast(I32),
-                )
+                rows = slice(SPREAD_START + SPREAD_STEP * r, spread_end, SPREAD_STEP * PLANE_ROWS)
+                nc.sync.dma_start(x_plane[r:P:QUADRANT, j0:g1].bitcast(I32), spread[rows, j0 - g0 :].bitcast(I32))
 
         spread_first = keep.tile([P, HALF], U8, name="spread_first", align_bytes=ALIGN)
-        pick_scales(0, spread_first)
-        nc.vector.quantize_mx(out=w_codes[:].bitcast(FP8X4), scales=w_plane[:], in_=w_grouped[:].rearrange("p m j -> p (m j)"))
-
-        window = late.tile([P, U], F32, name="window", align_bytes=DMA_ALIGN, offset=HALF)
-        spread_second = late.tile([P, HALF], U8, name="spread_second", align_bytes=ALIGN, offset=0)
-        nc.sync.dma_start(window[:], mem)
-        pick_scales(1, spread_second)
-        nc.gpsimd.tensor_scalar(cap[:, :CAP_VECTOR], fresh[:, :CAP_VECTOR], -1.0, 0.0, ALU.mult, ALU.add)
-        nc.scalar.activation(cap[:, CAP_VECTOR:], fresh[:, CAP_VECTOR:], COPY, scale=-1.0)
+        pick_scales(spread_first, 0, HALF, 0)
+        nc.vector.quantize_mx(
+            out=w_codes[:].bitcast(FP8X4),
+            scales=w_plane[:],
+            in_=w_grouped[:].rearrange("p m j -> p (m j)"),
+        )
+        window = after_weights.tile([P, U], F32, name="window", align_bytes=DMA_ALIGN, offset=HALF)
+        spread_second = after_weights.tile([P, HALF], U8, name="spread_second", align_bytes=ALIGN, offset=0)
+        mem_cols = [slice(c, c + U // MEM_PIECES) for c in range(0, U, U // MEM_PIECES)]
+        for cols in mem_cols:
+            nc.sync.dma_start(window[:, cols], mem[:, cols])
+        pick_scales(spread_second, HALF, S, HALF)
+        nc.gpsimd.tensor_scalar(cap[:, :CAP_GPSIMD], fresh[:, :CAP_GPSIMD], -1.0, 0.0, ALU.mult, ALU.add)
+        nc.scalar.activation(cap[:, CAP_GPSIMD:], fresh[:, CAP_GPSIMD:], COPY, scale=-1.0)
 
         picked = keep.tile([P, S], U32, name="picked", align_bytes=ALIGN)
-        for g0, g1 in GATHERS:
-            nc.vector.tensor_copy(picked[:, g0:g1], words[:].indirect(entries(offs_sb, g0, g1)))
+        for j0, j1 in ((0, FIRST), (FIRST, S)):
+            nc.vector.tensor_copy(picked[:, j0:j1], words[:].indirect(entries(offs_sb, j0, j1)))
 
         y_first = keep.tile([P, FIRST], F32, name="y_first", align_bytes=ALIGN)
         y_rest = keep.tile([P, S - FIRST], F32, name="y_rest", align_bytes=ALIGN)
-        for b, products in enumerate(BANKS):
+        for b, products in enumerate(FILLINGS):
             a0, a1 = products[0][0], products[-1][1]
             acc = psum.tile([P, BANK], F32, name="acc%d" % (b % 2))
             for j0, j1 in products:
@@ -128,14 +135,14 @@ def tile_picked_kvput_tanh_p_kernel(tc, x_words, x_scales, mem, w1, offs, slot, 
             nc.scalar.activation(y, acc[:, : a1 - a0], TANH)
             if a1 == FIRST:
                 nc.scalar.activation(fresh[:].indirect(entries(slot_sb, 0, FIRST)), y_first[:], COPY)
-        nc.scalar.activation(fresh[:].indirect(entries(slot_sb, FIRST, FIRST + LAST)), y_rest[:, :LAST], COPY)
+        nc.scalar.activation(fresh[:].indirect(entries(slot_sb, FIRST, SCALAR_END)), y_rest[:, :longest], COPY)
+
+        for cols in mem_cols:
+            nc.vector.tensor_tensor(window[:, cols], window[:, cols], cap[:, cols], ALU.min)
+        nc.vector.tensor_copy(window[:].indirect(entries(slot_sb, SCALAR_END, S)), y_rest[:, longest:])
 
         merged = keep.tile([P, U], F32, name="merged", align_bytes=DMA_ALIGN)
-        for kind, c0, c1 in TAIL:
-            if kind == "min":
-                nc.vector.tensor_tensor(window[:, c0:c1], window[:, c0:c1], cap[:, c0:c1], ALU.min)
-            elif kind == "scatter":
-                nc.vector.tensor_copy(window[:].indirect(entries(slot_sb, c0, c1)), y_rest[:, c0 - FIRST : c1 - FIRST])
-            else:
-                nc.vector.tensor_tensor(merged[:, c0:c1], window[:, c0:c1], fresh[:, c0:c1], ALU.max)
-                nc.sync.dma_start(out[:, c0:c1], merged[:, c0:c1])
+        for i, width in enumerate(STORES):
+            cols = slice(sum(STORES[:i]), sum(STORES[:i]) + width)
+            nc.vector.tensor_tensor(merged[:, cols], window[:, cols], fresh[:, cols], ALU.max)
+            nc.sync.dma_start(out[:, cols], merged[:, cols])

@@ -27,8 +27,7 @@ DMA_ALIGN = 256
 FLT_MAX = (2.0 - 2.0**-23) * 2.0**127
 MARK = 2.0
 
-SPREAD_START, SPREAD_STEP = 32, 4
-SCALE_ROWS = 16
+SPREAD_STEP = 8
 CLEAR_CUT, CLEAR_VECTOR = 209, 416
 FILL_CUT, FILL_VECTOR = 463, 928
 MARKS_SCALAR = 15
@@ -37,9 +36,11 @@ FIRST, SCALAR_END = 256, 640
 PIECES = ((0, FIRST), (FIRST, SCALAR_END), (SCALAR_END, S))
 HALF = S // 2
 FILLINGS = (((0, 128),), ((128, 256),), ((256, 512), (512, 640)), ((640, 896), (896, 1024)))
+WINDOW_AT = 4 * U
+CODES_AT = 8 * U
+SPREAD_AT = CODES_AT - DMA_ALIGN
 CAP_GPSIMD = 1088
-MEM_PIECES = 1
-STORES = (448, 448, 384, 384, 384)
+STORES = (512, 512, 512, 512)
 
 
 def tile_picked_kvput_tanh_p_kernel(tc, x_words, x_scales, mem, w1, offs, slot, out):
@@ -64,8 +65,7 @@ def tile_picked_kvput_tanh_p_kernel(tc, x_words, x_scales, mem, w1, offs, slot, 
         nc.sync.dma_start(slot_sb[:], slot)
         nc.sync.dma_start(w_raw[:], w1.rearrange("(p j) m -> p j m", j=PACK))
         nc.sync.dma_start(offs_sb[:], offs)
-        spread_end = SPREAD_START + SPREAD_STEP * SCALE_ROWS
-        nc.sync.dma_start(scales[SPREAD_START:spread_end:SPREAD_STEP, :].bitcast(I32), x_scales[0].bitcast(I32))
+        nc.sync.dma_start(scales[0:P:SPREAD_STEP, :].bitcast(I32), x_scales[0].bitcast(I32))
         nc.sync.dma_start(words[:].bitcast(I32), x_words[0].rearrange("p n t -> p (n t)").bitcast(I32))
 
         def entries(list_tile, j0, j1):
@@ -81,10 +81,9 @@ def tile_picked_kvput_tanh_p_kernel(tc, x_words, x_scales, mem, w1, offs, slot, 
         nc.vector.memset(fresh[:, :FILL_CUT], -FLT_MAX)
         nc.vector.memset(fresh[:, FILL_CUT:FILL_VECTOR], -FLT_MAX)
         nc.gpsimd.memset(fresh[:, FILL_VECTOR:], -FLT_MAX)
-        nc.vector.memset(x_plane[:].bitcast(I32), 0)
 
         w_grouped = after_weights.tile([P, N, PACK], BF16, name="w_grouped", align_bytes=ALIGN, offset=0)
-        w_codes = keep.tile([P, N], U32, name="w_codes", align_bytes=ALIGN)
+        w_codes = after_scales.tile([P, N], U32, name="w_codes", align_bytes=ALIGN, offset=CODES_AT)
         w_plane = keep.tile([P, N], U8, name="w_plane", align_bytes=ALIGN)
         nc.vector.tensor_copy(w_grouped[:], w_raw[:].rearrange("p j m -> p m j"))
         for j0, j1 in PIECES[:2]:
@@ -92,22 +91,23 @@ def tile_picked_kvput_tanh_p_kernel(tc, x_words, x_scales, mem, w1, offs, slot, 
 
         def pick_scales(spread, g0, g1, j0):
             nc.vector.tensor_copy(spread[:], scales[:].indirect(entries(offs_sb, g0, g1)))
-            for r in range(PLANE_ROWS):
-                rows = slice(SPREAD_START + SPREAD_STEP * r, spread_end, SPREAD_STEP * PLANE_ROWS)
-                nc.sync.dma_start(x_plane[r:P:QUADRANT, j0:g1].bitcast(I32), spread[rows, j0 - g0 :].bitcast(I32))
+            nc.vector.tensor_copy(x_plane[:, j0:g1].bitcast(I32), spread[:, j0 - g0 :].bitcast(I32))
+            for r in range(1, PLANE_ROWS):
+                nc.sync.dma_start(
+                    x_plane[r:P:QUADRANT, j0:g1].bitcast(I32),
+                    x_plane[SPREAD_STEP * r : P : QUADRANT, j0:g1].bitcast(I32),
+                )
 
-        spread_first = keep.tile([P, HALF], U8, name="spread_first", align_bytes=ALIGN)
+        spread_first = after_scales.tile([P, HALF], U8, name="spread_first", align_bytes=ALIGN, offset=SPREAD_AT)
         pick_scales(spread_first, 0, HALF, 0)
         nc.vector.quantize_mx(
             out=w_codes[:].bitcast(FP8X4),
             scales=w_plane[:],
             in_=w_grouped[:].rearrange("p m j -> p (m j)"),
         )
-        window = after_weights.tile([P, U], F32, name="window", align_bytes=DMA_ALIGN, offset=HALF)
+        window = after_scales.tile([P, U], F32, name="window", align_bytes=DMA_ALIGN, offset=WINDOW_AT)
         spread_second = after_weights.tile([P, HALF], U8, name="spread_second", align_bytes=ALIGN, offset=0)
-        mem_cols = [slice(c, c + U // MEM_PIECES) for c in range(0, U, U // MEM_PIECES)]
-        for cols in mem_cols:
-            nc.sync.dma_start(window[:, cols], mem[:, cols])
+        nc.sync.dma_start(window[:], mem)
         pick_scales(spread_second, HALF, S, HALF)
         nc.gpsimd.tensor_scalar(cap[:, :CAP_GPSIMD], fresh[:, :CAP_GPSIMD], -1.0, 0.0, ALU.mult, ALU.add)
         nc.scalar.activation(cap[:, CAP_GPSIMD:], fresh[:, CAP_GPSIMD:], COPY, scale=-1.0)
@@ -137,8 +137,7 @@ def tile_picked_kvput_tanh_p_kernel(tc, x_words, x_scales, mem, w1, offs, slot, 
                 nc.scalar.activation(fresh[:].indirect(entries(slot_sb, 0, FIRST)), y_first[:], COPY)
         nc.scalar.activation(fresh[:].indirect(entries(slot_sb, FIRST, SCALAR_END)), y_rest[:, :longest], COPY)
 
-        for cols in mem_cols:
-            nc.vector.tensor_tensor(window[:, cols], window[:, cols], cap[:, cols], ALU.min)
+        nc.vector.tensor_tensor(window[:], window[:], cap[:], ALU.min)
         nc.vector.tensor_copy(window[:].indirect(entries(slot_sb, SCALAR_END, S)), y_rest[:, longest:])
 
         merged = keep.tile([P, U], F32, name="merged", align_bytes=DMA_ALIGN)

@@ -24,22 +24,21 @@ STRIPE = 16
 BANK = 512
 ALIGN = 64
 DMA_ALIGN = 256
-FLT_MAX = (2.0 - 2.0**-23) * 2.0**127
-MARK = 2.0
 
 SPREAD_STEP = 8
 CLEAR_CUT, CLEAR_VECTOR = 209, 416
 FILL_CUT, FILL_VECTOR = 463, 928
 MARKS_SCALAR = 15
 
-FIRST, SCALAR_END = 256, 640
-PIECES = ((0, FIRST), (FIRST, SCALAR_END), (SCALAR_END, S))
+FIRST, VECTOR_END = 256, 672
+MARKS_CUT = 352
+FILLINGS = (((0, 128),), ((128, 256),), ((256, 512), (512, 640), (640, 704)), ((704, 960), (960, 1024)))
 HALF = S // 2
-FILLINGS = (((0, 128),), ((128, 256),), ((256, 512), (512, 640)), ((640, 896), (896, 1024)))
 WINDOW_AT = 4 * U
-CODES_AT = 8 * U
+CODES_AT = WINDOW_AT + 4 * U
 SPREAD_AT = CODES_AT - DMA_ALIGN
-CAP_GPSIMD = 1088
+CLEAR_GPSIMD = 640
+MASK_GPSIMD = 896
 STORES = (512, 512, 512, 512)
 
 
@@ -71,22 +70,21 @@ def tile_picked_kvput_tanh_p_kernel(tc, x_words, x_scales, mem, w1, offs, slot, 
         def entries(list_tile, j0, j1):
             return list_tile[:, j0 // STRIPE : j1 // STRIPE]
 
-        longest = SCALAR_END - FIRST
-        cap = after_scales.tile([P, U], F32, name="cap", align_bytes=ALIGN, offset=0)
-        marks = keep.tile([P, longest], F32, name="marks", align_bytes=ALIGN)
+        mask = after_scales.tile([P, U], F32, name="mask", align_bytes=ALIGN, offset=0)
+        marks = keep.tile([P, MARKS_CUT], F32, name="marks", align_bytes=ALIGN)
         fresh = keep.tile([P, U], F32, name="fresh", align_bytes=ALIGN)
         x_plane = keep.tile([P, S], U8, name="x_plane", align_bytes=ALIGN)
-        nc.vector.memset(marks[:, MARKS_SCALAR:], MARK)
+        nc.vector.memset(marks[:, MARKS_SCALAR:], 1.0)
         nc.scalar.activation(marks[:, :MARKS_SCALAR], marks[:, MARKS_SCALAR : 2 * MARKS_SCALAR], COPY)
-        nc.vector.memset(fresh[:, :FILL_CUT], -FLT_MAX)
-        nc.vector.memset(fresh[:, FILL_CUT:FILL_VECTOR], -FLT_MAX)
-        nc.gpsimd.memset(fresh[:, FILL_VECTOR:], -FLT_MAX)
+        nc.vector.memset(fresh[:, :FILL_CUT], 0.0)
+        nc.vector.memset(fresh[:, FILL_CUT:FILL_VECTOR], 0.0)
+        nc.gpsimd.memset(fresh[:, FILL_VECTOR:], 0.0)
 
         w_grouped = after_weights.tile([P, N, PACK], BF16, name="w_grouped", align_bytes=ALIGN, offset=0)
         w_codes = after_scales.tile([P, N], U32, name="w_codes", align_bytes=ALIGN, offset=CODES_AT)
         w_plane = keep.tile([P, N], U8, name="w_plane", align_bytes=ALIGN)
         nc.vector.tensor_copy(w_grouped[:], w_raw[:].rearrange("p j m -> p m j"))
-        for j0, j1 in PIECES[:2]:
+        for j0, j1 in ((0, MARKS_CUT), (MARKS_CUT, VECTOR_END)):
             nc.scalar.activation(fresh[:].indirect(entries(slot_sb, j0, j1)), marks[:, : j1 - j0], COPY)
 
         def pick_scales(spread, g0, g1, j0):
@@ -107,10 +105,12 @@ def tile_picked_kvput_tanh_p_kernel(tc, x_words, x_scales, mem, w1, offs, slot, 
         )
         window = after_scales.tile([P, U], F32, name="window", align_bytes=DMA_ALIGN, offset=WINDOW_AT)
         spread_second = after_weights.tile([P, HALF], U8, name="spread_second", align_bytes=ALIGN, offset=0)
-        nc.sync.dma_start(window[:], mem)
+        for cols in (slice(0, CLEAR_GPSIMD), slice(CLEAR_GPSIMD, U)):
+            nc.sync.dma_start(window[:, cols], mem[:, cols])
         pick_scales(spread_second, HALF, S, HALF)
-        nc.gpsimd.tensor_scalar(cap[:, :CAP_GPSIMD], fresh[:, :CAP_GPSIMD], -1.0, 0.0, ALU.mult, ALU.add)
-        nc.scalar.activation(cap[:, CAP_GPSIMD:], fresh[:, CAP_GPSIMD:], COPY, scale=-1.0)
+        nc.gpsimd.tensor_scalar(mask[:, :MASK_GPSIMD], fresh[:, :MASK_GPSIMD], -1.0, 1.0, ALU.mult, ALU.add)
+        nc.scalar.activation(mask[:, MASK_GPSIMD:], fresh[:, MASK_GPSIMD:], COPY, bias=1.0, scale=-1.0)
+        nc.gpsimd.tensor_tensor(window[:, :CLEAR_GPSIMD], window[:, :CLEAR_GPSIMD], mask[:, :CLEAR_GPSIMD], ALU.mult)
 
         picked = keep.tile([P, S], U32, name="picked", align_bytes=ALIGN)
         for j0, j1 in ((0, FIRST), (FIRST, S)):
@@ -135,13 +135,13 @@ def tile_picked_kvput_tanh_p_kernel(tc, x_words, x_scales, mem, w1, offs, slot, 
             nc.scalar.activation(y, acc[:, : a1 - a0], TANH)
             if a1 == FIRST:
                 nc.scalar.activation(fresh[:].indirect(entries(slot_sb, 0, FIRST)), y_first[:], COPY)
-        nc.scalar.activation(fresh[:].indirect(entries(slot_sb, FIRST, SCALAR_END)), y_rest[:, :longest], COPY)
 
-        nc.vector.tensor_tensor(window[:], window[:], cap[:], ALU.min)
-        nc.vector.tensor_copy(window[:].indirect(entries(slot_sb, SCALAR_END, S)), y_rest[:, longest:])
+        nc.vector.tensor_tensor(window[:, CLEAR_GPSIMD:], window[:, CLEAR_GPSIMD:], mask[:, CLEAR_GPSIMD:], ALU.mult)
+        nc.vector.tensor_copy(fresh[:].indirect(entries(slot_sb, FIRST, VECTOR_END)), y_rest[:, : VECTOR_END - FIRST])
+        nc.scalar.activation(window[:].indirect(entries(slot_sb, VECTOR_END, S)), y_rest[:, VECTOR_END - FIRST :], COPY)
 
         merged = keep.tile([P, U], F32, name="merged", align_bytes=DMA_ALIGN)
         for i, width in enumerate(STORES):
             cols = slice(sum(STORES[:i]), sum(STORES[:i]) + width)
-            nc.vector.tensor_tensor(merged[:, cols], window[:, cols], fresh[:, cols], ALU.max)
+            nc.vector.tensor_tensor(merged[:, cols], window[:, cols], fresh[:, cols], ALU.add)
             nc.sync.dma_start(out[:, cols], merged[:, cols])

@@ -32,7 +32,7 @@ MARKS_SCALAR = 15
 
 FIRST, VECTOR_END = 256, 672
 MARKS_CUT = 352
-FILLINGS = (((0, 128),), ((128, 256),), ((256, 512), (512, 640), (640, 704)), ((704, 960), (960, 1024)))
+FILLINGS = (((0, 128),), ((128, 256),), ((256, 320),), ((320, 576), (576, 704)), ((704, 960), (960, 1024)))
 HALF = S // 2
 WINDOW_AT = 4 * U
 CODES_AT = WINDOW_AT + 4 * U
@@ -113,14 +113,14 @@ def tile_picked_kvput_tanh_p_kernel(tc, x_words, x_scales, mem, w1, offs, slot, 
         nc.gpsimd.tensor_tensor(window[:, :CLEAR_GPSIMD], window[:, :CLEAR_GPSIMD], mask[:, :CLEAR_GPSIMD], ALU.mult)
 
         picked = keep.tile([P, S], U32, name="picked", align_bytes=ALIGN)
-        for j0, j1 in ((0, FIRST), (FIRST, S)):
+        for j0, j1 in ((0, FIRST), (FIRST, HALF), (HALF, S)):
             nc.vector.tensor_copy(picked[:, j0:j1], words[:].indirect(entries(offs_sb, j0, j1)))
 
         y_first = keep.tile([P, FIRST], F32, name="y_first", align_bytes=ALIGN)
         y_rest = keep.tile([P, S - FIRST], F32, name="y_rest", align_bytes=ALIGN)
         for b, products in enumerate(FILLINGS):
             a0, a1 = products[0][0], products[-1][1]
-            acc = psum.tile([P, BANK], F32, name="acc%d" % (b % 2))
+            acc = psum.tile([P, BANK], F32, name="acc%d" % (b % 3))
             for j0, j1 in products:
                 nc.tensor.matmul_mx(
                     out=acc[:, j0 - a0 : j1 - a0],
@@ -133,7 +133,7 @@ def tile_picked_kvput_tanh_p_kernel(tc, x_words, x_scales, mem, w1, offs, slot, 
                 )
             y = y_first[:, a0:a1] if a1 <= FIRST else y_rest[:, a0 - FIRST : a1 - FIRST]
             nc.scalar.activation(y, acc[:, : a1 - a0], TANH)
-            if a1 == FIRST:
+            if a1 == FIRST + ALIGN:
                 nc.scalar.activation(fresh[:].indirect(entries(slot_sb, 0, FIRST)), y_first[:], COPY)
 
         nc.vector.tensor_tensor(window[:, CLEAR_GPSIMD:], window[:, CLEAR_GPSIMD:], mask[:, CLEAR_GPSIMD:], ALU.mult)

@@ -30,15 +30,14 @@ CLEAR_CUT, CLEAR_VECTOR = 209, 416
 FILL_CUT, FILL_VECTOR = 463, 928
 MARKS_SCALAR = 15
 
-FIRST, VECTOR_END = 256, 672
-MARKS_CUT = 352
+FIRST, EARLY_END, VECTOR_END = 256, 320, 704
+MARKS_CUT = 320
 FILLINGS = (((0, 128),), ((128, 256),), ((256, 320),), ((320, 576), (576, 704)), ((704, 960), (960, 1024)))
 HALF = S // 2
 WINDOW_AT = 4 * U
 CODES_AT = WINDOW_AT + 4 * U
 SPREAD_AT = CODES_AT - DMA_ALIGN
 CLEAR_GPSIMD = 640
-MASK_GPSIMD = 896
 STORES = (512, 512, 512, 512)
 
 
@@ -70,7 +69,8 @@ def tile_picked_kvput_tanh_p_kernel(tc, x_words, x_scales, mem, w1, offs, slot, 
         def entries(list_tile, j0, j1):
             return list_tile[:, j0 // STRIPE : j1 // STRIPE]
 
-        mask = after_scales.tile([P, U], F32, name="mask", align_bytes=ALIGN, offset=0)
+        mask_g = after_scales.tile([P, CLEAR_GPSIMD], F32, name="mask_g", align_bytes=ALIGN, offset=0)
+        mask_v = after_scales.tile([P, U - CLEAR_GPSIMD], F32, name="mask_v", align_bytes=ALIGN, offset=4 * CLEAR_GPSIMD)
         marks = keep.tile([P, MARKS_CUT], F32, name="marks", align_bytes=ALIGN)
         fresh = keep.tile([P, U], F32, name="fresh", align_bytes=ALIGN)
         x_plane = keep.tile([P, S], U8, name="x_plane", align_bytes=ALIGN)
@@ -84,20 +84,19 @@ def tile_picked_kvput_tanh_p_kernel(tc, x_words, x_scales, mem, w1, offs, slot, 
         w_codes = after_scales.tile([P, N], U32, name="w_codes", align_bytes=ALIGN, offset=CODES_AT)
         w_plane = keep.tile([P, N], U8, name="w_plane", align_bytes=ALIGN)
         nc.vector.tensor_copy(w_grouped[:], w_raw[:].rearrange("p j m -> p m j"))
-        for j0, j1 in ((0, MARKS_CUT), (MARKS_CUT, VECTOR_END)):
+        for j0, j1 in ((0, EARLY_END), (VECTOR_END, S)):
             nc.scalar.activation(fresh[:].indirect(entries(slot_sb, j0, j1)), marks[:, : j1 - j0], COPY)
 
-        def pick_scales(spread, g0, g1, j0):
+        def pick_scales(spread, g0, g1, in_plane):
             nc.vector.tensor_copy(spread[:], scales[:].indirect(entries(offs_sb, g0, g1)))
-            nc.vector.tensor_copy(x_plane[:, j0:g1].bitcast(I32), spread[:, j0 - g0 :].bitcast(I32))
+            nc.vector.tensor_copy(x_plane[:, g0:g1].bitcast(I32), spread[:].bitcast(I32))
             for r in range(1, PLANE_ROWS):
-                nc.sync.dma_start(
-                    x_plane[r:P:QUADRANT, j0:g1].bitcast(I32),
-                    x_plane[SPREAD_STEP * r : P : QUADRANT, j0:g1].bitcast(I32),
-                )
+                rows = slice(SPREAD_STEP * r, P, QUADRANT)
+                source = x_plane[rows, g0:g1] if in_plane else spread[rows, :]
+                nc.sync.dma_start(x_plane[r:P:QUADRANT, g0:g1].bitcast(I32), source.bitcast(I32))
 
         spread_first = after_scales.tile([P, HALF], U8, name="spread_first", align_bytes=ALIGN, offset=SPREAD_AT)
-        pick_scales(spread_first, 0, HALF, 0)
+        pick_scales(spread_first, 0, HALF, True)
         nc.vector.quantize_mx(
             out=w_codes[:].bitcast(FP8X4),
             scales=w_plane[:],
@@ -107,10 +106,12 @@ def tile_picked_kvput_tanh_p_kernel(tc, x_words, x_scales, mem, w1, offs, slot, 
         spread_second = after_weights.tile([P, HALF], U8, name="spread_second", align_bytes=ALIGN, offset=0)
         for cols in (slice(0, CLEAR_GPSIMD), slice(CLEAR_GPSIMD, U)):
             nc.sync.dma_start(window[:, cols], mem[:, cols])
-        pick_scales(spread_second, HALF, S, HALF)
-        nc.gpsimd.tensor_scalar(mask[:, :MASK_GPSIMD], fresh[:, :MASK_GPSIMD], -1.0, 1.0, ALU.mult, ALU.add)
-        nc.scalar.activation(mask[:, MASK_GPSIMD:], fresh[:, MASK_GPSIMD:], COPY, bias=1.0, scale=-1.0)
-        nc.gpsimd.tensor_tensor(window[:, :CLEAR_GPSIMD], window[:, :CLEAR_GPSIMD], mask[:, :CLEAR_GPSIMD], ALU.mult)
+        pick_scales(spread_second, HALF, S, False)
+        nc.gpsimd.tensor_scalar(mask_g[:], fresh[:, :CLEAR_GPSIMD], -1.0, 1.0, ALU.mult, ALU.add)
+        nc.scalar.activation(mask_v[:], fresh[:, CLEAR_GPSIMD:], COPY, bias=1.0, scale=-1.0)
+        nc.gpsimd.tensor_tensor(window[:, :CLEAR_GPSIMD], window[:, :CLEAR_GPSIMD], mask_g[:], ALU.mult)
+        zeros = after_weights.tile([P, EARLY_END - FIRST], F32, name="zeros", align_bytes=ALIGN, offset=0)
+        nc.gpsimd.memset(zeros[:], 0.0)
 
         picked = keep.tile([P, S], U32, name="picked", align_bytes=ALIGN)
         for j0, j1 in ((0, FIRST), (FIRST, HALF), (HALF, S)):
@@ -136,9 +137,14 @@ def tile_picked_kvput_tanh_p_kernel(tc, x_words, x_scales, mem, w1, offs, slot, 
             if a1 == FIRST + ALIGN:
                 nc.scalar.activation(fresh[:].indirect(entries(slot_sb, 0, FIRST)), y_first[:], COPY)
 
-        nc.vector.tensor_tensor(window[:, CLEAR_GPSIMD:], window[:, CLEAR_GPSIMD:], mask[:, CLEAR_GPSIMD:], ALU.mult)
-        nc.vector.tensor_copy(fresh[:].indirect(entries(slot_sb, FIRST, VECTOR_END)), y_rest[:, : VECTOR_END - FIRST])
-        nc.scalar.activation(window[:].indirect(entries(slot_sb, VECTOR_END, S)), y_rest[:, VECTOR_END - FIRST :], COPY)
+        nc.vector.tensor_tensor(window[:, CLEAR_GPSIMD:], window[:, CLEAR_GPSIMD:], mask_v[:], ALU.mult)
+        nc.vector.tensor_tensor(
+            fresh[:].indirect(entries(slot_sb, FIRST, EARLY_END)), y_rest[:, : EARLY_END - FIRST], zeros[:], ALU.add
+        )
+        nc.vector.tensor_copy(
+            window[:].indirect(entries(slot_sb, EARLY_END, VECTOR_END)), y_rest[:, EARLY_END - FIRST : VECTOR_END - FIRST]
+        )
+        nc.scalar.activation(fresh[:].indirect(entries(slot_sb, VECTOR_END, S)), y_rest[:, VECTOR_END - FIRST :], COPY)
 
         merged = keep.tile([P, U], F32, name="merged", align_bytes=DMA_ALIGN)
         for i, width in enumerate(STORES):

@@ -1,6 +1,7 @@
 from contextlib import ExitStack
 
 import concourse.mybir as mybir
+from concourse.masks import make_identity
 
 K, T, S, N, U = 512, 4096, 1024, 128, 2048
 FLOPS = 2 * K * N * S
@@ -37,7 +38,8 @@ HALF = S // 2
 WINDOW_AT = 4 * U
 CODES_AT = WINDOW_AT + 4 * U
 SPREAD_AT = CODES_AT - DMA_ALIGN
-CLEAR_GPSIMD = 640
+CLEAR_GPSIMD = 1024
+BLOCKS = BANK // P
 STORES = (512, 512, 512, 512)
 
 
@@ -70,7 +72,6 @@ def tile_picked_kvput_tanh_p_kernel(tc, x_words, x_scales, mem, w1, offs, slot, 
             return list_tile[:, j0 // STRIPE : j1 // STRIPE]
 
         mask_g = after_scales.tile([P, CLEAR_GPSIMD], F32, name="mask_g", align_bytes=ALIGN, offset=0)
-        mask_v = after_scales.tile([P, U - CLEAR_GPSIMD], F32, name="mask_v", align_bytes=ALIGN, offset=4 * CLEAR_GPSIMD)
         marks = keep.tile([P, MARKS_CUT], F32, name="marks", align_bytes=ALIGN)
         fresh = keep.tile([P, U], F32, name="fresh", align_bytes=ALIGN)
         x_plane = keep.tile([P, S], U8, name="x_plane", align_bytes=ALIGN)
@@ -79,6 +80,8 @@ def tile_picked_kvput_tanh_p_kernel(tc, x_words, x_scales, mem, w1, offs, slot, 
         nc.vector.memset(fresh[:, :FILL_CUT], 0.0)
         nc.vector.memset(fresh[:, FILL_CUT:FILL_VECTOR], 0.0)
         nc.gpsimd.memset(fresh[:, FILL_VECTOR:], 0.0)
+        identity = keep.tile([P, P], F32, name="identity", align_bytes=ALIGN)
+        make_identity(nc, identity[:])
 
         w_grouped = after_weights.tile([P, N, PACK], BF16, name="w_grouped", align_bytes=ALIGN, offset=0)
         w_codes = after_scales.tile([P, N], U32, name="w_codes", align_bytes=ALIGN, offset=CODES_AT)
@@ -108,10 +111,18 @@ def tile_picked_kvput_tanh_p_kernel(tc, x_words, x_scales, mem, w1, offs, slot, 
             nc.sync.dma_start(window[:, cols], mem[:, cols])
         pick_scales(spread_second, HALF, S, False)
         nc.gpsimd.tensor_scalar(mask_g[:], fresh[:, :CLEAR_GPSIMD], -1.0, 1.0, ALU.mult, ALU.add)
-        nc.scalar.activation(mask_v[:], fresh[:, CLEAR_GPSIMD:], COPY, bias=1.0, scale=-1.0)
         nc.gpsimd.tensor_tensor(window[:, :CLEAR_GPSIMD], window[:, :CLEAR_GPSIMD], mask_g[:], ALU.mult)
         zeros = after_weights.tile([P, EARLY_END - FIRST], F32, name="zeros", align_bytes=ALIGN, offset=0)
         nc.gpsimd.memset(zeros[:], 0.0)
+
+        mask_banks = (U - CLEAR_GPSIMD) // BANK
+        mask_down = keep.tile([P, mask_banks * BLOCKS], F32, name="mask_down", align_bytes=ALIGN)
+        for b in range(mask_banks):
+            turned = psum.tile([P, BANK], F32, name="acc%d" % (3 + b))
+            for i in range(BLOCKS):
+                c = CLEAR_GPSIMD + b * BANK + i * P
+                nc.tensor.transpose(turned[:, i * P : (i + 1) * P], fresh[:, c : c + P], identity[:])
+            nc.scalar.activation(mask_down[:, b * BLOCKS : (b + 1) * BLOCKS], turned[:, 0:BANK:P], COPY, bias=1.0, scale=-1.0)
 
         picked = keep.tile([P, S], U32, name="picked", align_bytes=ALIGN)
         for j0, j1 in ((0, FIRST), (FIRST, HALF), (HALF, S)):
@@ -121,7 +132,7 @@ def tile_picked_kvput_tanh_p_kernel(tc, x_words, x_scales, mem, w1, offs, slot, 
         y_rest = keep.tile([P, S - FIRST], F32, name="y_rest", align_bytes=ALIGN)
         for b, products in enumerate(FILLINGS):
             a0, a1 = products[0][0], products[-1][1]
-            acc = psum.tile([P, BANK], F32, name="acc%d" % (b % 3))
+            acc = psum.tile([P, BANK], F32, name="acc%d" % b)
             for j0, j1 in products:
                 nc.tensor.matmul_mx(
                     out=acc[:, j0 - a0 : j1 - a0],
@@ -136,8 +147,14 @@ def tile_picked_kvput_tanh_p_kernel(tc, x_words, x_scales, mem, w1, offs, slot, 
             nc.scalar.activation(y, acc[:, : a1 - a0], TANH)
             if a1 == FIRST + ALIGN:
                 nc.scalar.activation(fresh[:].indirect(entries(slot_sb, 0, FIRST)), y_first[:], COPY)
+                for m in range(mask_banks):
+                    mask_v = psum.tile([P, BANK], F32, name="acc%d" % m)
+                    for i in range(BLOCKS):
+                        column = mask_down[:, m * BLOCKS + i : m * BLOCKS + i + 1]
+                        nc.tensor.transpose(mask_v[:, i * P : (i + 1) * P], column.to_broadcast([P, P]), identity[:])
+                    cols = slice(CLEAR_GPSIMD + m * BANK, CLEAR_GPSIMD + (m + 1) * BANK)
+                    nc.vector.tensor_tensor(window[:, cols], window[:, cols], mask_v[:], ALU.mult)
 
-        nc.vector.tensor_tensor(window[:, CLEAR_GPSIMD:], window[:, CLEAR_GPSIMD:], mask_v[:], ALU.mult)
         nc.vector.tensor_tensor(
             fresh[:].indirect(entries(slot_sb, FIRST, EARLY_END)), y_rest[:, : EARLY_END - FIRST], zeros[:], ALU.add
         )

@@ -33,14 +33,16 @@ MARKS_SCALAR = 15
 
 FIRST, EARLY_END, VECTOR_END = 256, 320, 704
 MARKS_CUT = 320
-FILLINGS = (((0, 128),), ((128, 256),), ((256, 320),), ((320, 576), (576, 704)), ((704, 960), (960, 1024)))
+FILLINGS = (((0, 128),), ((128, 256),), ((256, 320),), ((320, 448), (448, 512), (512, 640), (640, 704)), ((704, 960), (960, 1024)))
 HALF = S // 2
 WINDOW_AT = 4 * U
 CODES_AT = WINDOW_AT + 4 * U
 SPREAD_AT = CODES_AT - DMA_ALIGN
-CLEAR_GPSIMD = 1024
-BLOCKS = BANK // P
-STORES = (512, 512, 512, 512)
+CLEAR_GPSIMD = 832
+CLEAR_BESIDE = CLEAR_GPSIMD + 512
+BLOCKS = 2
+PART = BLOCKS * P
+STORES = (384, 512, 576, 576)
 
 
 def tile_picked_kvput_tanh_p_kernel(tc, x_words, x_scales, mem, w1, offs, slot, out):
@@ -72,6 +74,7 @@ def tile_picked_kvput_tanh_p_kernel(tc, x_words, x_scales, mem, w1, offs, slot, 
             return list_tile[:, j0 // STRIPE : j1 // STRIPE]
 
         mask_g = after_scales.tile([P, CLEAR_GPSIMD], F32, name="mask_g", align_bytes=ALIGN, offset=0)
+        mask_s = after_scales.tile([P, U - CLEAR_BESIDE], F32, name="mask_s", align_bytes=ALIGN, offset=4 * CLEAR_GPSIMD)
         marks = keep.tile([P, MARKS_CUT], F32, name="marks", align_bytes=ALIGN)
         fresh = keep.tile([P, U], F32, name="fresh", align_bytes=ALIGN)
         x_plane = keep.tile([P, S], U8, name="x_plane", align_bytes=ALIGN)
@@ -82,6 +85,8 @@ def tile_picked_kvput_tanh_p_kernel(tc, x_words, x_scales, mem, w1, offs, slot, 
         nc.gpsimd.memset(fresh[:, FILL_VECTOR:], 0.0)
         identity = keep.tile([P, P], F32, name="identity", align_bytes=ALIGN)
         make_identity(nc, identity[:])
+        identity_bf16 = keep.tile([P, P], BF16, name="identity_bf16", align_bytes=ALIGN)
+        make_identity(nc, identity_bf16[:])
 
         w_grouped = after_weights.tile([P, N, PACK], BF16, name="w_grouped", align_bytes=ALIGN, offset=0)
         w_codes = after_scales.tile([P, N], U32, name="w_codes", align_bytes=ALIGN, offset=CODES_AT)
@@ -111,18 +116,19 @@ def tile_picked_kvput_tanh_p_kernel(tc, x_words, x_scales, mem, w1, offs, slot, 
             nc.sync.dma_start(window[:, cols], mem[:, cols])
         pick_scales(spread_second, HALF, S, False)
         nc.gpsimd.tensor_scalar(mask_g[:], fresh[:, :CLEAR_GPSIMD], -1.0, 1.0, ALU.mult, ALU.add)
+        nc.scalar.activation(mask_s[:], fresh[:, CLEAR_BESIDE:], COPY, bias=1.0, scale=-1.0)
         nc.gpsimd.tensor_tensor(window[:, :CLEAR_GPSIMD], window[:, :CLEAR_GPSIMD], mask_g[:], ALU.mult)
         zeros = after_weights.tile([P, EARLY_END - FIRST], F32, name="zeros", align_bytes=ALIGN, offset=0)
         nc.gpsimd.memset(zeros[:], 0.0)
 
-        mask_banks = (U - CLEAR_GPSIMD) // BANK
-        mask_down = keep.tile([P, mask_banks * BLOCKS], F32, name="mask_down", align_bytes=ALIGN)
+        mask_banks = (CLEAR_BESIDE - CLEAR_GPSIMD) // PART
+        mask_down = keep.tile([P, mask_banks * BLOCKS], BF16, name="mask_down", align_bytes=ALIGN)
         for b in range(mask_banks):
             turned = psum.tile([P, BANK], F32, name="acc%d" % (3 + b))
             for i in range(BLOCKS):
-                c = CLEAR_GPSIMD + b * BANK + i * P
+                c = CLEAR_GPSIMD + b * PART + i * P
                 nc.tensor.transpose(turned[:, i * P : (i + 1) * P], fresh[:, c : c + P], identity[:])
-            nc.scalar.activation(mask_down[:, b * BLOCKS : (b + 1) * BLOCKS], turned[:, 0:BANK:P], COPY, bias=1.0, scale=-1.0)
+            nc.scalar.activation(mask_down[:, b * BLOCKS : (b + 1) * BLOCKS], turned[:, 0:PART:P], COPY, bias=1.0, scale=-1.0)
 
         picked = keep.tile([P, S], U32, name="picked", align_bytes=ALIGN)
         for j0, j1 in ((0, FIRST), (FIRST, HALF), (HALF, S)):
@@ -148,13 +154,14 @@ def tile_picked_kvput_tanh_p_kernel(tc, x_words, x_scales, mem, w1, offs, slot, 
             if a1 == FIRST + ALIGN:
                 nc.scalar.activation(fresh[:].indirect(entries(slot_sb, 0, FIRST)), y_first[:], COPY)
                 for m in range(mask_banks):
-                    mask_v = psum.tile([P, BANK], F32, name="acc%d" % m)
+                    mask_v = psum.tile([P, BANK], BF16, name="acc%d" % m)
                     for i in range(BLOCKS):
                         column = mask_down[:, m * BLOCKS + i : m * BLOCKS + i + 1]
-                        nc.tensor.transpose(mask_v[:, i * P : (i + 1) * P], column.to_broadcast([P, P]), identity[:])
-                    cols = slice(CLEAR_GPSIMD + m * BANK, CLEAR_GPSIMD + (m + 1) * BANK)
-                    nc.vector.tensor_tensor(window[:, cols], window[:, cols], mask_v[:], ALU.mult)
+                        nc.tensor.transpose(mask_v[:, i * P : (i + 1) * P], column.to_broadcast([P, P]), identity_bf16[:])
+                    cols = slice(CLEAR_GPSIMD + m * PART, CLEAR_GPSIMD + (m + 1) * PART)
+                    nc.vector.tensor_tensor(window[:, cols], window[:, cols], mask_v[:, :PART], ALU.mult)
 
+        nc.vector.tensor_tensor(window[:, CLEAR_BESIDE:], window[:, CLEAR_BESIDE:], mask_s[:], ALU.mult)
         nc.vector.tensor_tensor(
             fresh[:].indirect(entries(slot_sb, FIRST, EARLY_END)), y_rest[:, : EARLY_END - FIRST], zeros[:], ALU.add
         )

@@ -1,7 +1,6 @@
 from contextlib import ExitStack
 
 import concourse.mybir as mybir
-from concourse.masks import make_identity
 
 K, T, S, N, U = 512, 4096, 1024, 128, 2048
 FLOPS = 2 * K * N * S
@@ -32,16 +31,13 @@ FILL_CUT, FILL_VECTOR = 463, 928
 MARKS_SCALAR = 15
 
 FIRST, EARLY_END, VECTOR_END = 256, 320, 704
-MARKS_CUT = 320
 FILLINGS = (((0, 128),), ((128, 256),), ((256, 320),), ((320, 448), (448, 512), (512, 640), (640, 704)), ((704, 960), (960, 1024)))
 HALF = S // 2
+G1, V1 = 512, 832
+MASK_CUT = 1088
 WINDOW_AT = 4 * U
 CODES_AT = WINDOW_AT + 4 * U
 SPREAD_AT = CODES_AT - DMA_ALIGN
-CLEAR_GPSIMD = 832
-CLEAR_BESIDE = CLEAR_GPSIMD + 512
-BLOCKS = 2
-PART = BLOCKS * P
 STORES = (384, 512, 576, 576)
 
 
@@ -73,9 +69,8 @@ def tile_picked_kvput_tanh_p_kernel(tc, x_words, x_scales, mem, w1, offs, slot, 
         def entries(list_tile, j0, j1):
             return list_tile[:, j0 // STRIPE : j1 // STRIPE]
 
-        mask_g = after_scales.tile([P, CLEAR_GPSIMD], F32, name="mask_g", align_bytes=ALIGN, offset=0)
-        mask_s = after_scales.tile([P, U - CLEAR_BESIDE], F32, name="mask_s", align_bytes=ALIGN, offset=4 * CLEAR_GPSIMD)
-        marks = keep.tile([P, MARKS_CUT], F32, name="marks", align_bytes=ALIGN)
+        mask = after_scales.tile([P, U], F32, name="mask", align_bytes=ALIGN, offset=0)
+        marks = keep.tile([P, EARLY_END], F32, name="marks", align_bytes=ALIGN)
         fresh = keep.tile([P, U], F32, name="fresh", align_bytes=ALIGN)
         x_plane = keep.tile([P, S], U8, name="x_plane", align_bytes=ALIGN)
         nc.vector.memset(marks[:, MARKS_SCALAR:], 1.0)
@@ -83,10 +78,6 @@ def tile_picked_kvput_tanh_p_kernel(tc, x_words, x_scales, mem, w1, offs, slot, 
         nc.vector.memset(fresh[:, :FILL_CUT], 0.0)
         nc.vector.memset(fresh[:, FILL_CUT:FILL_VECTOR], 0.0)
         nc.gpsimd.memset(fresh[:, FILL_VECTOR:], 0.0)
-        identity = keep.tile([P, P], F32, name="identity", align_bytes=ALIGN)
-        make_identity(nc, identity[:])
-        identity_bf16 = keep.tile([P, P], BF16, name="identity_bf16", align_bytes=ALIGN)
-        make_identity(nc, identity_bf16[:])
 
         w_grouped = after_weights.tile([P, N, PACK], BF16, name="w_grouped", align_bytes=ALIGN, offset=0)
         w_codes = after_scales.tile([P, N], U32, name="w_codes", align_bytes=ALIGN, offset=CODES_AT)
@@ -112,27 +103,20 @@ def tile_picked_kvput_tanh_p_kernel(tc, x_words, x_scales, mem, w1, offs, slot, 
         )
         window = after_scales.tile([P, U], F32, name="window", align_bytes=DMA_ALIGN, offset=WINDOW_AT)
         spread_second = after_weights.tile([P, HALF], U8, name="spread_second", align_bytes=ALIGN, offset=0)
-        for cols in (slice(0, CLEAR_GPSIMD), slice(CLEAR_GPSIMD, U)):
-            nc.sync.dma_start(window[:, cols], mem[:, cols])
+        nc.sync.dma_start(window[:, :V1], mem[:, :V1])
+        nc.sync.dma_start(window[:, V1:], mem[:, V1:])
         pick_scales(spread_second, HALF, S, False)
-        nc.gpsimd.tensor_scalar(mask_g[:], fresh[:, :CLEAR_GPSIMD], -1.0, 1.0, ALU.mult, ALU.add)
-        nc.scalar.activation(mask_s[:], fresh[:, CLEAR_BESIDE:], COPY, bias=1.0, scale=-1.0)
-        nc.gpsimd.tensor_tensor(window[:, :CLEAR_GPSIMD], window[:, :CLEAR_GPSIMD], mask_g[:], ALU.mult)
+        nc.gpsimd.tensor_scalar(mask[:, :MASK_CUT], fresh[:, :MASK_CUT], -1.0, 1.0, ALU.mult, ALU.add)
+        nc.scalar.activation(mask[:, MASK_CUT:], fresh[:, MASK_CUT:], COPY, bias=1.0, scale=-1.0)
+        nc.gpsimd.tensor_tensor(window[:, :G1], window[:, :G1], mask[:, :G1], ALU.mult)
         zeros = after_weights.tile([P, EARLY_END - FIRST], F32, name="zeros", align_bytes=ALIGN, offset=0)
         nc.gpsimd.memset(zeros[:], 0.0)
-
-        mask_banks = (CLEAR_BESIDE - CLEAR_GPSIMD) // PART
-        mask_down = keep.tile([P, mask_banks * BLOCKS], BF16, name="mask_down", align_bytes=ALIGN)
-        for b in range(mask_banks):
-            turned = psum.tile([P, BANK], F32, name="acc%d" % (3 + b))
-            for i in range(BLOCKS):
-                c = CLEAR_GPSIMD + b * PART + i * P
-                nc.tensor.transpose(turned[:, i * P : (i + 1) * P], fresh[:, c : c + P], identity[:])
-            nc.scalar.activation(mask_down[:, b * BLOCKS : (b + 1) * BLOCKS], turned[:, 0:PART:P], COPY, bias=1.0, scale=-1.0)
 
         picked = keep.tile([P, S], U32, name="picked", align_bytes=ALIGN)
         for j0, j1 in ((0, FIRST), (FIRST, HALF), (HALF, S)):
             nc.vector.tensor_copy(picked[:, j0:j1], words[:].indirect(entries(offs_sb, j0, j1)))
+        nc.vector.tensor_tensor(window[:, G1:V1], window[:, G1:V1], mask[:, G1:V1], ALU.mult)
+        nc.vector.tensor_tensor(window[:, V1:], window[:, V1:], mask[:, V1:], ALU.mult)
 
         y_first = keep.tile([P, FIRST], F32, name="y_first", align_bytes=ALIGN)
         y_rest = keep.tile([P, S - FIRST], F32, name="y_rest", align_bytes=ALIGN)
@@ -151,17 +135,9 @@ def tile_picked_kvput_tanh_p_kernel(tc, x_words, x_scales, mem, w1, offs, slot, 
                 )
             y = y_first[:, a0:a1] if a1 <= FIRST else y_rest[:, a0 - FIRST : a1 - FIRST]
             nc.scalar.activation(y, acc[:, : a1 - a0], TANH)
-            if a1 == FIRST + ALIGN:
+            if a1 == EARLY_END:
                 nc.scalar.activation(fresh[:].indirect(entries(slot_sb, 0, FIRST)), y_first[:], COPY)
-                for m in range(mask_banks):
-                    mask_v = psum.tile([P, BANK], BF16, name="acc%d" % m)
-                    for i in range(BLOCKS):
-                        column = mask_down[:, m * BLOCKS + i : m * BLOCKS + i + 1]
-                        nc.tensor.transpose(mask_v[:, i * P : (i + 1) * P], column.to_broadcast([P, P]), identity_bf16[:])
-                    cols = slice(CLEAR_GPSIMD + m * PART, CLEAR_GPSIMD + (m + 1) * PART)
-                    nc.vector.tensor_tensor(window[:, cols], window[:, cols], mask_v[:, :PART], ALU.mult)
 
-        nc.vector.tensor_tensor(window[:, CLEAR_BESIDE:], window[:, CLEAR_BESIDE:], mask_s[:], ALU.mult)
         nc.vector.tensor_tensor(
             fresh[:].indirect(entries(slot_sb, FIRST, EARLY_END)), y_rest[:, : EARLY_END - FIRST], zeros[:], ALU.add
         )

@@ -33,7 +33,7 @@ MARKS_SCALAR = 15
 FIRST, EARLY_END, VECTOR_END = 256, 320, 704
 FILLINGS = (((0, 128),), ((128, 256),), ((256, 320),), ((320, 448), (448, 512), (512, 640), (640, 704)), ((704, 960), (960, 1024)))
 HALF = S // 2
-G1, V1 = 512, 832
+G1, V1 = 448, 832
 MASK_CUT = 1088
 WINDOW_AT = 4 * U
 CODES_AT = WINDOW_AT + 4 * U
@@ -103,20 +103,22 @@ def tile_picked_kvput_tanh_p_kernel(tc, x_words, x_scales, mem, w1, offs, slot, 
         )
         window = after_scales.tile([P, U], F32, name="window", align_bytes=DMA_ALIGN, offset=WINDOW_AT)
         spread_second = after_weights.tile([P, HALF], U8, name="spread_second", align_bytes=ALIGN, offset=0)
-        nc.sync.dma_start(window[:, :V1], mem[:, :V1])
-        nc.sync.dma_start(window[:, V1:], mem[:, V1:])
+        staged = keep.tile([P, U - V1], F32, name="staged", align_bytes=DMA_ALIGN)
+        nc.sync.dma_start(window[:, G1 : G1 + V1], mem[:, :V1])
+        nc.sync.dma_start(staged[:], mem[:, V1:])
         pick_scales(spread_second, HALF, S, False)
         nc.gpsimd.tensor_scalar(mask[:, :MASK_CUT], fresh[:, :MASK_CUT], -1.0, 1.0, ALU.mult, ALU.add)
         nc.scalar.activation(mask[:, MASK_CUT:], fresh[:, MASK_CUT:], COPY, bias=1.0, scale=-1.0)
-        nc.gpsimd.tensor_tensor(window[:, :G1], window[:, :G1], mask[:, :G1], ALU.mult)
+        nc.gpsimd.tensor_tensor(window[:, :G1], window[:, G1 : 2 * G1], mask[:, :G1], ALU.mult)
         zeros = after_weights.tile([P, EARLY_END - FIRST], F32, name="zeros", align_bytes=ALIGN, offset=0)
         nc.gpsimd.memset(zeros[:], 0.0)
 
         picked = keep.tile([P, S], U32, name="picked", align_bytes=ALIGN)
         for j0, j1 in ((0, FIRST), (FIRST, HALF), (HALF, S)):
             nc.vector.tensor_copy(picked[:, j0:j1], words[:].indirect(entries(offs_sb, j0, j1)))
-        nc.vector.tensor_tensor(window[:, G1:V1], window[:, G1:V1], mask[:, G1:V1], ALU.mult)
-        nc.vector.tensor_tensor(window[:, V1:], window[:, V1:], mask[:, V1:], ALU.mult)
+        nc.vector.tensor_tensor(window[:, G1:V1], window[:, 2 * G1 : G1 + V1], mask[:, G1:V1], ALU.mult)
+        for c0, c1 in ((G1 + V1, U), (V1, G1 + V1)):
+            nc.vector.tensor_tensor(window[:, c0:c1], staged[:, c0 - V1 : c1 - V1], mask[:, c0:c1], ALU.mult)
 
         y_first = keep.tile([P, FIRST], F32, name="y_first", align_bytes=ALIGN)
         y_rest = keep.tile([P, S - FIRST], F32, name="y_rest", align_bytes=ALIGN)

@@ -27,18 +27,18 @@ DMA_ALIGN = 256
 
 SPREAD_STEP = 8
 CLEAR_CUT, CLEAR_VECTOR = 209, 416
-FILL_CUT, FILL_VECTOR = 463, 928
+FILL_CUT, FILL_VECTOR = 351, 704
 MARKS_SCALAR = 15
 
-FIRST, EARLY_END, VECTOR_END = 256, 320, 704
-FILLINGS = (((0, 128),), ((128, 256),), ((256, 320),), ((320, 448), (448, 512), (512, 640), (640, 704)), ((704, 960), (960, 1024)))
+FIRST, EARLY_END, FRESH_END = 256, 320, 640
+FILLINGS = (((0, 128),), ((128, 256),), ((256, 320),), ((640, 896), (896, 1024)), ((320, 448), (448, 512), (512, 640)))
 HALF = S // 2
 G1, V1 = 448, 832
-MASK_CUT = 1088
+MASK_CUT = 896
 WINDOW_AT = 4 * U
 CODES_AT = WINDOW_AT + 4 * U
 SPREAD_AT = CODES_AT - DMA_ALIGN
-STORES = (384, 512, 576, 576)
+STORES = (576, 704, 768)
 
 
 def tile_picked_kvput_tanh_p_kernel(tc, x_words, x_scales, mem, w1, offs, slot, out):
@@ -70,7 +70,7 @@ def tile_picked_kvput_tanh_p_kernel(tc, x_words, x_scales, mem, w1, offs, slot, 
             return list_tile[:, j0 // STRIPE : j1 // STRIPE]
 
         mask = after_scales.tile([P, U], F32, name="mask", align_bytes=ALIGN, offset=0)
-        marks = keep.tile([P, EARLY_END], F32, name="marks", align_bytes=ALIGN)
+        marks = keep.tile([P, FRESH_END], F32, name="marks", align_bytes=ALIGN)
         fresh = keep.tile([P, U], F32, name="fresh", align_bytes=ALIGN)
         x_plane = keep.tile([P, S], U8, name="x_plane", align_bytes=ALIGN)
         nc.vector.memset(marks[:, MARKS_SCALAR:], 1.0)
@@ -83,8 +83,8 @@ def tile_picked_kvput_tanh_p_kernel(tc, x_words, x_scales, mem, w1, offs, slot, 
         w_codes = after_scales.tile([P, N], U32, name="w_codes", align_bytes=ALIGN, offset=CODES_AT)
         w_plane = keep.tile([P, N], U8, name="w_plane", align_bytes=ALIGN)
         nc.vector.tensor_copy(w_grouped[:], w_raw[:].rearrange("p j m -> p m j"))
-        for j0, j1 in ((0, EARLY_END), (VECTOR_END, S)):
-            nc.scalar.activation(fresh[:].indirect(entries(slot_sb, j0, j1)), marks[:, : j1 - j0], COPY)
+        one = marks[:, MARKS_SCALAR : MARKS_SCALAR + 1]
+        nc.scalar.activation(fresh[:].indirect(entries(slot_sb, 0, FRESH_END)), marks[:], COPY, scale=one)
 
         def pick_scales(spread, g0, g1, in_plane):
             nc.vector.tensor_copy(spread[:], scales[:].indirect(entries(offs_sb, g0, g1)))
@@ -143,10 +143,10 @@ def tile_picked_kvput_tanh_p_kernel(tc, x_words, x_scales, mem, w1, offs, slot, 
         nc.vector.tensor_tensor(
             fresh[:].indirect(entries(slot_sb, FIRST, EARLY_END)), y_rest[:, : EARLY_END - FIRST], zeros[:], ALU.add
         )
-        nc.vector.tensor_copy(
-            window[:].indirect(entries(slot_sb, EARLY_END, VECTOR_END)), y_rest[:, EARLY_END - FIRST : VECTOR_END - FIRST]
+        nc.vector.tensor_copy(window[:].indirect(entries(slot_sb, FRESH_END, S)), y_rest[:, FRESH_END - FIRST :])
+        nc.scalar.activation(
+            fresh[:].indirect(entries(slot_sb, EARLY_END, FRESH_END)), y_rest[:, EARLY_END - FIRST : FRESH_END - FIRST], COPY
         )
-        nc.scalar.activation(fresh[:].indirect(entries(slot_sb, VECTOR_END, S)), y_rest[:, VECTOR_END - FIRST :], COPY)
 
         merged = keep.tile([P, U], F32, name="merged", align_bytes=DMA_ALIGN)
         for i, width in enumerate(STORES):

from contextlib import ExitStack

import concourse.mybir as mybir

K, T, S, N, U = 512, 4096, 1024, 128, 2048
FLOPS = 2 * K * N * S

F32 = mybir.dt.float32
BF16 = mybir.dt.bfloat16
I32 = mybir.dt.int32
U32 = mybir.dt.uint32
U16 = mybir.dt.uint16
U8 = mybir.dt.uint8
FP8X4 = mybir.dt.float8_e4m3fn_x4
TANH = mybir.ActivationFunctionType.Tanh
COPY = mybir.ActivationFunctionType.Copy
ALU = mybir.AluOpType

P = 128
PACK = 4
QUADRANT = 32
PLANE_ROWS = 4
STRIPE = 16
BANK = 512
ALIGN = 64
DMA_ALIGN = 256

SPREAD_STEP = 8
CLEAR_CUT, CLEAR_VECTOR = 209, 416
FILL_CUT, FILL_VECTOR = 351, 704
MARKS_SCALAR = 15

FIRST, EARLY_END, FRESH_END = 256, 320, 640
FILLINGS = (((0, 128),), ((128, 256),), ((256, 320),), ((640, 896), (896, 1024)), ((320, 448), (448, 512), (512, 640)))
HALF = S // 2
G1, V1 = 448, 832
MASK_CUT = 896
WINDOW_AT = 4 * U
CODES_AT = WINDOW_AT + 4 * U
SPREAD_AT = CODES_AT - DMA_ALIGN
STORES = (576, 704, 768)


def tile_picked_kvput_tanh_p_kernel(tc, x_words, x_scales, mem, w1, offs, slot, out):
    nc = tc.nc
    with ExitStack() as ctx:
        keep = ctx.enter_context(tc.tile_pool(name="keep", bufs=1))
        after_scales = ctx.enter_context(tc.tile_pool(name="after_scales", bufs=1))
        after_weights = ctx.enter_context(tc.tile_pool(name="after_weights", bufs=1))
        psum = ctx.enter_context(tc.psum_pool(name="psum", bufs=1))

        offs_sb = keep.tile([P, S // STRIPE], U16, name="offs_sb")
        slot_sb = keep.tile([P, S // STRIPE], U16, name="slot_sb")
        words = keep.tile([P, T], U32, name="words", align_bytes=DMA_ALIGN)
        scales = after_scales.tile([P, T], U8, name="scales", align_bytes=DMA_ALIGN, offset=0)
        w_raw = keep.tile([P, PACK, N], F32, name="w_raw", align_bytes=DMA_ALIGN)

        scale_words = scales[:].bitcast(I32)
        nc.vector.memset(scale_words[:, :CLEAR_CUT], 0)
        nc.vector.memset(scale_words[:, CLEAR_CUT:CLEAR_VECTOR], 0)
        nc.gpsimd.memset(scale_words[:, CLEAR_VECTOR:], 0)

        nc.sync.dma_start(slot_sb[:], slot)
        nc.sync.dma_start(w_raw[:], w1.rearrange("(p j) m -> p j m", j=PACK))
        nc.sync.dma_start(offs_sb[:], offs)
        nc.sync.dma_start(scales[0:P:SPREAD_STEP, :].bitcast(I32), x_scales[0].bitcast(I32))
        nc.sync.dma_start(words[:].bitcast(I32), x_words[0].rearrange("p n t -> p (n t)").bitcast(I32))

        def entries(list_tile, j0, j1):
            return list_tile[:, j0 // STRIPE : j1 // STRIPE]

        mask = after_scales.tile([P, U], F32, name="mask", align_bytes=ALIGN, offset=0)
        marks = keep.tile([P, FRESH_END], F32, name="marks", align_bytes=ALIGN)
        fresh = keep.tile([P, U], F32, name="fresh", align_bytes=ALIGN)
        x_plane = keep.tile([P, S], U8, name="x_plane", align_bytes=ALIGN)
        nc.vector.memset(marks[:, MARKS_SCALAR:], 1.0)
        nc.scalar.activation(marks[:, :MARKS_SCALAR], marks[:, MARKS_SCALAR : 2 * MARKS_SCALAR], COPY)
        nc.vector.memset(fresh[:, :FILL_CUT], 0.0)
        nc.vector.memset(fresh[:, FILL_CUT:FILL_VECTOR], 0.0)
        nc.gpsimd.memset(fresh[:, FILL_VECTOR:], 0.0)

        w_grouped = after_weights.tile([P, N, PACK], BF16, name="w_grouped", align_bytes=ALIGN, offset=0)
        w_codes = after_scales.tile([P, N], U32, name="w_codes", align_bytes=ALIGN, offset=CODES_AT)
        w_plane = keep.tile([P, N], U8, name="w_plane", align_bytes=ALIGN)
        nc.vector.tensor_copy(w_grouped[:], w_raw[:].rearrange("p j m -> p m j"))
        one = marks[:, MARKS_SCALAR : MARKS_SCALAR + 1]
        nc.scalar.activation(fresh[:].indirect(entries(slot_sb, 0, FRESH_END)), marks[:], COPY, scale=one)

        def pick_scales(spread, g0, g1, in_plane):
            nc.vector.tensor_copy(spread[:], scales[:].indirect(entries(offs_sb, g0, g1)))
            nc.vector.tensor_copy(x_plane[:, g0:g1].bitcast(I32), spread[:].bitcast(I32))
            for r in range(1, PLANE_ROWS):
                rows = slice(SPREAD_STEP * r, P, QUADRANT)
                source = x_plane[rows, g0:g1] if in_plane else spread[rows, :]
                nc.sync.dma_start(x_plane[r:P:QUADRANT, g0:g1].bitcast(I32), source.bitcast(I32))

        spread_first = after_scales.tile([P, HALF], U8, name="spread_first", align_bytes=ALIGN, offset=SPREAD_AT)
        pick_scales(spread_first, 0, HALF, True)
        nc.vector.quantize_mx(
            out=w_codes[:].bitcast(FP8X4),
            scales=w_plane[:],
            in_=w_grouped[:].rearrange("p m j -> p (m j)"),
        )
        window = after_scales.tile([P, U], F32, name="window", align_bytes=DMA_ALIGN, offset=WINDOW_AT)
        spread_second = after_weights.tile([P, HALF], U8, name="spread_second", align_bytes=ALIGN, offset=0)
        staged = keep.tile([P, U - V1], F32, name="staged", align_bytes=DMA_ALIGN)
        nc.sync.dma_start(window[:, G1 : G1 + V1], mem[:, :V1])
        nc.sync.dma_start(staged[:], mem[:, V1:])
        pick_scales(spread_second, HALF, S, False)
        nc.gpsimd.tensor_scalar(mask[:, :MASK_CUT], fresh[:, :MASK_CUT], -1.0, 1.0, ALU.mult, ALU.add)
        nc.scalar.activation(mask[:, MASK_CUT:], fresh[:, MASK_CUT:], COPY, bias=1.0, scale=-1.0)
        nc.gpsimd.tensor_tensor(window[:, :G1], window[:, G1 : 2 * G1], mask[:, :G1], ALU.mult)
        zeros = after_weights.tile([P, EARLY_END - FIRST], F32, name="zeros", align_bytes=ALIGN, offset=0)
        nc.gpsimd.memset(zeros[:], 0.0)

        picked = keep.tile([P, S], U32, name="picked", align_bytes=ALIGN)
        for j0, j1 in ((0, FIRST), (FIRST, HALF), (HALF, S)):
            nc.vector.tensor_copy(picked[:, j0:j1], words[:].indirect(entries(offs_sb, j0, j1)))
        nc.vector.tensor_tensor(window[:, G1:V1], window[:, 2 * G1 : G1 + V1], mask[:, G1:V1], ALU.mult)
        for c0, c1 in ((G1 + V1, U), (V1, G1 + V1)):
            nc.vector.tensor_tensor(window[:, c0:c1], staged[:, c0 - V1 : c1 - V1], mask[:, c0:c1], ALU.mult)

        y_first = keep.tile([P, FIRST], F32, name="y_first", align_bytes=ALIGN)
        y_rest = keep.tile([P, S - FIRST], F32, name="y_rest", align_bytes=ALIGN)
        for b, products in enumerate(FILLINGS):
            a0, a1 = products[0][0], products[-1][1]
            acc = psum.tile([P, BANK], F32, name="acc%d" % b)
            for j0, j1 in products:
                nc.tensor.matmul_mx(
                    out=acc[:, j0 - a0 : j1 - a0],
                    lhsT=w_codes[:].bitcast(FP8X4),
                    lhsT_scale=w_plane[:],
                    rhs=picked[:, j0:j1].bitcast(FP8X4),
                    rhs_scale=x_plane[:, j0:j1],
                    start=True,
                    stop=True,
                )
            y = y_first[:, a0:a1] if a1 <= FIRST else y_rest[:, a0 - FIRST : a1 - FIRST]
            nc.scalar.activation(y, acc[:, : a1 - a0], TANH)
            if a1 == EARLY_END:
                nc.scalar.activation(fresh[:].indirect(entries(slot_sb, 0, FIRST)), y_first[:], COPY)

        nc.vector.tensor_tensor(
            fresh[:].indirect(entries(slot_sb, FIRST, EARLY_END)), y_rest[:, : EARLY_END - FIRST], zeros[:], ALU.add
        )
        nc.vector.tensor_copy(window[:].indirect(entries(slot_sb, FRESH_END, S)), y_rest[:, FRESH_END - FIRST :])
        nc.scalar.activation(
            fresh[:].indirect(entries(slot_sb, EARLY_END, FRESH_END)), y_rest[:, EARLY_END - FIRST : FRESH_END - FIRST], COPY
        )

        merged = keep.tile([P, U], F32, name="merged", align_bytes=DMA_ALIGN)
        for i, width in enumerate(STORES):
            cols = slice(sum(STORES[:i]), sum(STORES[:i]) + width)
            nc.vector.tensor_tensor(merged[:, cols], window[:, cols], fresh[:, cols], ALU.add)
            nc.sync.dma_start(out[:, cols], merged[:, cols])
